import numpy as np
import ml_dtypes


def mxq(x, axis, fmt="e4m3"):
    dtype, down = {"e4m3": (ml_dtypes.float8_e4m3fn, 7), "e5m2": (ml_dtypes.float8_e5m2, 14)}[fmt]
    v = np.moveaxis(np.asarray(x, np.float32).astype(ml_dtypes.bfloat16).astype(np.float64), axis, -1)
    blocks = v.reshape(v.shape[:-1] + (-1, 32))
    amax = np.abs(blocks).max(-1, keepdims=True)
    byte = np.maximum(np.where(amax > 0, np.frexp(amax)[1] - 1 + 127, 0) - down, 1)
    scale = np.exp2(byte - 127.0)
    codes = (blocks / scale).astype(np.float32).astype(dtype).astype(np.float64)
    return np.moveaxis((codes * scale).reshape(v.shape), -1, axis)


WIDE = False


def mx_kscale(k):
    if not WIDE:
        return np.ones(k)
    levels = np.array([10, -10, 5, -5, 0])
    if k % 512:
        return np.exp2(np.random.permutation(np.resize(levels, k // 32))).repeat(32)
    a = np.empty((k // 512, 16))
    for p in range(k // 512):
        a[p, :8] = np.random.permutation(np.resize(levels, 8))
        for g in range(8):
            far = levels[np.abs(levels - a[p, g]) >= 10]
            a[p, g + 8] = far[np.random.randint(len(far))]
    return np.exp2(a.ravel()).repeat(32)


def f64(x):
    return np.asarray(x).astype(np.float64)


def striped(idx):
    return np.tile(idx.reshape(-1, 16).T, (8, 1)).astype(np.uint16)


def unstriped(offs):
    return offs[:16].T.reshape(-1).astype(np.int64)


E2M1 = np.array([0.0, 0.5, 1.0, 1.5, 2.0, 3.0, 4.0, 6.0, -0.0, -0.5, -1.0, -1.5, -2.0, -3.0, -4.0, -6.0])


def pack_weight(w, fmt):
    k, n = w.shape
    w = f64(np.asarray(w, np.float32).astype(ml_dtypes.bfloat16)).reshape(k // 32, 32, n)
    amax = np.abs(w).max(1)
    if fmt == "e4m3":
        byte = np.frexp(amax)[1] - 1 + 127 - 7
    else:
        mant, ex = np.frexp(amax / 6.0)
        byte = np.where(mant > 0.5, ex, ex - 1) + 127
    byte = np.clip(np.where(amax > 0, byte, 1), 1, 254)
    scaled = (w * np.exp2(127.0 - byte)[:, None, :]).reshape(k, n).astype(np.float32)
    by_word = np.ascontiguousarray(scaled.reshape(k // 512, 128, 4, n).transpose(0, 1, 3, 2))
    if fmt == "e4m3":
        words = by_word.astype(ml_dtypes.float8_e4m3fn).view(np.uint8)
    else:
        c = by_word.astype(ml_dtypes.float4_e2m1fn).view(np.uint8) & 0xF
        words = (c[..., 0::2] | (c[..., 1::2] << 4)).reshape(k // 512, 128, 2 * n)
    return np.ascontiguousarray(words), np.ascontiguousarray(byte.astype(np.uint8).reshape(k // 512, 16, n))


def unpack_weight(words, scales, fmt):
    g, _, n = scales.shape
    words = np.ascontiguousarray(words).reshape(g, 128, n, -1)
    if fmt == "e4m3":
        vals = words.view(ml_dtypes.float8_e4m3fn).astype(np.float64)
    else:
        nib = np.empty((g, 128, n, 4), np.uint8)
        nib[..., 0::2] = words & 0xF
        nib[..., 1::2] = words >> 4
        vals = E2M1[nib]
    vals = vals * np.repeat(np.exp2(scales.astype(np.float64) - 127.0), 8, axis=1)[..., None]
    return vals.transpose(0, 1, 3, 2).reshape(g * 512, n)


def gelu(v):
    return 0.5 * v * (1.0 + np.tanh(np.sqrt(2.0 / np.pi) * (v + 0.044715 * v**3)))


K, M, T, S = 512, 128, 4096, 1536


def setup_inputs():
    n = np.random.standard_normal
    s = mx_kscale(K)[:, None]
    u = mx_kscale(512)[:, None]
    v = pack_weight(n((K, T)) * s, "e4m3")
    p_w2 = pack_weight(1.4 * n((512, M)) / np.sqrt(512) / u, "e2m1")
    return {
        "tab_words": v[0],
        "tab_scales": v[1],
        "w1": (n((K, 512)) / np.sqrt(K) / s * u.T).astype(np.float32),
        "w2_words": p_w2[0],
        "w2_scales": p_w2[1],
        "gT": n((M, T)).astype(np.float32),
        "b": (0.3 * n(128)).astype(np.float32),
        "offs": striped(np.random.permutation(T)[:S]),
    }


def reference(tab_words, tab_scales, w1, w2_words, w2_scales, gT, b, offs):
    tab_ = unpack_weight(tab_words, tab_scales, "e4m3")[:, unstriped(offs)]
    w1_ = mxq(f64(w1), 0, "e4m3")
    w2_ = unpack_weight(w2_words, w2_scales, "e2m1")
    h_ = mxq(np.maximum(w1_.T @ tab_, 0.0), 0, "e4m3")
    y = w2_.T @ h_
    return (gelu(y + f64(b)[:, None])) * f64(gT)[:, unstriped(offs)]

@@ -1,0 +1,173 @@
+from contextlib import ExitStack
+
+import concourse.mybir as mybir
+
+K, M, T, S, H = 512, 128, 4096, 1536, 512
+FLOPS = 2 * K * H * S + 2 * H * M * S
+
+F32 = mybir.dt.float32
+BF16 = mybir.dt.bfloat16
+I32 = mybir.dt.int32
+U32 = mybir.dt.uint32
+U16 = mybir.dt.uint16
+U8 = mybir.dt.uint8
+FP8X4 = mybir.dt.float8_e4m3fn_x4
+FP4X4 = mybir.dt.float4_e2m1fn_x4
+ACT = mybir.ActivationFunctionType
+ALU = mybir.AluOpType
+
+P = 128
+PACK = 4
+UNIT = 128
+GATHER = 512
+W1_PIECES = [(0, 128), (128, 256), (256, 384), (384, 512)]
+GROUPS = [(0, 2), (2, 4), (4, 6), (6, 8), (8, 10), (10, 11), (11, 12)]
+VECTOR_UNITS = (3, 5, 8)
+LAG = 3
+
+
+def tile_list_tabgate_gelu_kernel(tc, tab_words, tab_scales, w1, w2_words, w2_scales, gT, b, offs, out):
+    nc = tc.nc
+    with ExitStack() as ctx:
+        held = ctx.enter_context(tc.tile_pool(name="held", bufs=1))
+        h_psum = ctx.enter_context(tc.psum_pool(name="h_psum", bufs=5))
+        y_psum = ctx.enter_context(tc.psum_pool(name="y_psum", bufs=3))
+
+        offsets = held.tile([P, S // 16], U16, name="offsets")
+        table_words = held.tile([P, T], I32, name="table_words", align_bytes=64)
+        table_scales = held.tile([P, T // 4], I32, name="table_scales", align_bytes=64)
+        gates = held.tile([P, T], F32, name="gates", align_bytes=64)
+        w2_codes = held.tile([P, 2 * M], U8, name="w2_codes", align_bytes=64)
+        w2_plane = held.tile([P, M // 4], I32, name="w2_plane", align_bytes=64)
+        bias = held.tile([P, 1], F32, name="bias")
+        warm_in = held.tile([P, 1], F32, name="warm_in")
+        warm_out = held.tile([P, 1], F32, name="warm_out")
+        w1_raw = [held.tile([P, PACK, c1 - c0], F32, name=f"w1_raw{c0}", align_bytes=64) for c0, c1 in W1_PIECES]
+        w1_grouped = held.tile([P, PACK, P, PACK], BF16, name="w1_grouped", tag="w1_then_words", align_bytes=64)
+        w1_codes = held.tile([P, H], U32, name="w1_codes", align_bytes=64)
+        w1_plane = held.tile([P, H], U8, name="w1_plane", align_bytes=64)
+        picked_words = [held.tile([P, GATHER], U32, name=f"picked_words{c}", align_bytes=64) for c in range(S // GATHER - 1)]
+        picked_plane = held.tile([P, S], U8, name="picked_plane", align_bytes=64)
+
+        nc.vector.memset(table_scales[:], 0)
+        nc.vector.memset(w2_plane[:], 0)
+        nc.gpsimd.memset(warm_in[:], 0.0)
+        nc.scalar.activation(warm_out[:], warm_in[:], ACT.Gelu_apprx_tanh)
+
+        w1_rows = w1.rearrange("(p j) c -> p j c", j=PACK)
+        tab_scale_rows = tab_scales[0].bitcast(I32)
+        w2_scale_rows = w2_scales[0].bitcast(I32)
+
+        def load_w1(i):
+            c0, c1 = W1_PIECES[i]
+            nc.sync.dma_start(w1_raw[i][:], w1_rows[:, :, c0:c1])
+
+        nc.sync.dma_start(offsets[:], offs)
+        nc.sync.dma_start(w2_codes[:].bitcast(I32), w2_words[0].bitcast(I32))
+        load_w1(0)
+        for r in range(4):
+            nc.sync.dma_start(table_scales[r:P:32, :], tab_scale_rows[r:16:4, :])
+        nc.sync.dma_start(table_words[:], tab_words[0].rearrange("p n t -> p (n t)").bitcast(I32))
+        load_w1(1)
+        load_w1(2)
+        load_w1(3)
+        for r in range(4):
+            nc.sync.dma_start(w2_plane[r:P:32, :], w2_scale_rows[r:16:4, :])
+        nc.sync.dma_start(gates[:], gT)
+        nc.gpsimd.dma_start(bias[:], b.rearrange("(p o) -> p o", o=1))
+
+        for i, (c0, c1) in enumerate(W1_PIECES):
+            nc.scalar.copy(
+                w1_grouped[:, :, c0 // PACK : c1 // PACK, :].rearrange("p t m j -> p m j t"),
+                w1_raw[i][:].rearrange("p j (m t) -> p m j t", t=PACK),
+            )
+
+        nc.vector.tensor_copy(picked_plane[:], table_scales[:].bitcast(U8).indirect(offsets[:]))
+
+        def list_slice(s0, s1):
+            return offsets[:, s0 // 16 : s1 // 16]
+
+        def gather_words(c):
+            nc.vector.tensor_copy(
+                picked_words[c][:], table_words[:].bitcast(U32).indirect(list_slice(c * GATHER, (c + 1) * GATHER))
+            )
+
+        gather_words(0)
+        gather_words(1)
+        for t in range(PACK):
+            cols = slice(t * P, (t + 1) * P)
+            nc.vector.quantize_mx(
+                out=w1_codes[:, cols].bitcast(FP8X4),
+                scales=w1_plane[:, cols],
+                in_=w1_grouped[:, t, :, :].rearrange("p m j -> p (m j)"),
+            )
+        picked_words.append(held.tile([P, GATHER], U32, name="picked_words_last", tag="w1_then_words", align_bytes=64))
+        gather_words(2)
+
+        h_grouped = [held.tile([P, (u1 - u0) * UNIT, PACK], BF16, name=f"h_grouped{u0}", align_bytes=64) for u0, u1 in GROUPS]
+        h_codes = {}
+        h_plane = [held.tile([P, (u1 - u0) * UNIT], U8, name=f"h_plane{u0}", align_bytes=64) for u0, u1 in GROUPS]
+        result = [held.tile([P, (u1 - u0) * UNIT], F32, name=f"result{u0}", align_bytes=64) for u0, u1 in GROUPS]
+        y_banks = {}
+
+        def first_layer(g):
+            u0, u1 = GROUPS[g]
+            for u in range(u0, u1):
+                c, s0 = divmod(u * UNIT, GATHER)
+                bank = h_psum.tile([P, PACK, UNIT], F32, name="h_bank")
+                for t in range(PACK):
+                    cols = slice(t * P, (t + 1) * P)
+                    nc.tensor.matmul_mx(
+                        out=bank[:, t, :],
+                        lhsT=w1_codes[:, cols].bitcast(FP8X4),
+                        lhsT_scale=w1_plane[:, cols],
+                        rhs=picked_words[c][:, s0 : s0 + UNIT].bitcast(FP8X4),
+                        rhs_scale=picked_plane[:, u * UNIT : (u + 1) * UNIT],
+                        start=True,
+                        stop=True,
+                    )
+                dst = h_grouped[g][:, (u - u0) * UNIT : (u - u0 + 1) * UNIT, :]
+                src = bank[:].rearrange("p t n -> p n t")
+                if u in VECTOR_UNITS:
+                    nc.vector.tensor_scalar_max(dst, src, 0.0)
+                else:
+                    nc.scalar.activation(dst, src, ACT.Relu)
+
+        def quantize_h(g):
+            u0, u1 = GROUPS[g]
+            h_codes[g] = held.tile([P, (u1 - u0) * UNIT], U32, name=f"h_codes{g}", tag=f"shared{g}", align_bytes=64)
+            nc.vector.quantize_mx(
+                out=h_codes[g][:].bitcast(FP8X4),
+                scales=h_plane[g][:],
+                in_=h_grouped[g][:].rearrange("p n t -> p (n t)"),
+            )
+
+        def second_layer(g):
+            u0, u1 = GROUPS[g]
+            y_banks[g] = y_psum.tile([P, (u1 - u0) * UNIT], F32, name="y_bank")
+            nc.tensor.matmul_mx(
+                out=y_banks[g][:],
+                lhsT=w2_codes[:].bitcast(FP4X4),
+                lhsT_scale=w2_plane[:].bitcast(U8),
+                rhs=h_codes[g][:].bitcast(FP8X4),
+                rhs_scale=h_plane[g][:],
+                start=True,
+                stop=True,
+            )
+
+        def finish(g):
+            u0, u1 = GROUPS[g]
+            activated = held.tile([P, (u1 - u0) * UNIT], F32, name=f"activated{g}", tag=f"shared{g + LAG}", align_bytes=64)
+            nc.scalar.activation(activated[:], y_banks[g][:], ACT.Gelu_apprx_tanh, bias=bias[:])
+            nc.vector.tensor_tensor(
+                result[g][:], gates[:].indirect(list_slice(u0 * UNIT, u1 * UNIT)), activated[:], ALU.mult
+            )
+            nc.sync.dma_start(out[:, u0 * UNIT : u1 * UNIT], result[g][:])
+
+        for g in range(len(GROUPS) + LAG):
+            if g >= LAG:
+                finish(g - LAG)
+            if g < len(GROUPS):
+                first_layer(g)
+                quantize_h(g)
+                second_layer(g)

@@ -20,18 +20,22 @@ P = 128
 PACK = 4
 UNIT = 128
 GATHER = 512
-W1_PIECES = [(0, 128), (128, 256), (256, 384), (384, 512)]
+W1_PIECES = [(0, 256), (256, 384), (384, 512)]
 GROUPS = [(0, 2), (2, 4), (4, 6), (6, 8), (8, 10), (10, 11), (11, 12)]
-VECTOR_UNITS = (3, 5, 8)
-LAG = 3
+VECTOR_UNITS = (2, 4, 6)
+SECOND_LAG = 3
+FINISH_LAG = 3
+REUSE_LAG = 4
+H_BANKS = 5
+HALF = P // 2
 
 
 def tile_list_tabgate_gelu_kernel(tc, tab_words, tab_scales, w1, w2_words, w2_scales, gT, b, offs, out):
     nc = tc.nc
     with ExitStack() as ctx:
         held = ctx.enter_context(tc.tile_pool(name="held", bufs=1))
-        h_psum = ctx.enter_context(tc.psum_pool(name="h_psum", bufs=5))
-        y_psum = ctx.enter_context(tc.psum_pool(name="y_psum", bufs=3))
+        h_psum = ctx.enter_context(tc.psum_pool(name="h_psum", bufs=H_BANKS))
+        y_psum = ctx.enter_context(tc.psum_pool(name="y_psum", bufs=8 - H_BANKS))
 
         offsets = held.tile([P, S // 16], U16, name="offsets")
         table_words = held.tile([P, T], I32, name="table_words", align_bytes=64)
@@ -68,9 +72,8 @@ def tile_list_tabgate_gelu_kernel(tc, tab_words, tab_scales, w1, w2_words, w2_sc
         for r in range(4):
             nc.sync.dma_start(table_scales[r:P:32, :], tab_scale_rows[r:16:4, :])
         nc.sync.dma_start(table_words[:], tab_words[0].rearrange("p n t -> p (n t)").bitcast(I32))
-        load_w1(1)
-        load_w1(2)
-        load_w1(3)
+        for i in range(1, len(W1_PIECES)):
+            load_w1(i)
         for r in range(4):
             nc.sync.dma_start(w2_plane[r:P:32, :], w2_scale_rows[r:16:4, :])
         nc.sync.dma_start(gates[:], gT)
@@ -92,15 +95,19 @@ def tile_list_tabgate_gelu_kernel(tc, tab_words, tab_scales, w1, w2_words, w2_sc
                 picked_words[c][:], table_words[:].bitcast(U32).indirect(list_slice(c * GATHER, (c + 1) * GATHER))
             )
 
+        def quantize_w1(m0):
+            for t in range(PACK):
+                cols = slice(t * P + m0, t * P + m0 + HALF)
+                nc.vector.quantize_mx(
+                    out=w1_codes[:, cols].bitcast(FP8X4),
+                    scales=w1_plane[:, cols],
+                    in_=w1_grouped[:, t, m0 : m0 + HALF, :].rearrange("p m j -> p (m j)"),
+                )
+
+        quantize_w1(0)
         gather_words(0)
         gather_words(1)
-        for t in range(PACK):
-            cols = slice(t * P, (t + 1) * P)
-            nc.vector.quantize_mx(
-                out=w1_codes[:, cols].bitcast(FP8X4),
-                scales=w1_plane[:, cols],
-                in_=w1_grouped[:, t, :, :].rearrange("p m j -> p (m j)"),
-            )
+        quantize_w1(HALF)
         picked_words.append(held.tile([P, GATHER], U32, name="picked_words_last", tag="w1_then_words", align_bytes=64))
         gather_words(2)
 
@@ -110,9 +117,10 @@ def tile_list_tabgate_gelu_kernel(tc, tab_words, tab_scales, w1, w2_words, w2_sc
         result = [held.tile([P, (u1 - u0) * UNIT], F32, name=f"result{u0}", align_bytes=64) for u0, u1 in GROUPS]
         y_banks = {}
 
-        def first_layer(g):
-            u0, u1 = GROUPS[g]
-            for u in range(u0, u1):
+        def first_layer(u):
+            g = [u0 <= u < u1 for u0, u1 in GROUPS].index(True)
+            u0 = GROUPS[g][0]
+            if True:
                 c, s0 = divmod(u * UNIT, GATHER)
                 bank = h_psum.tile([P, PACK, UNIT], F32, name="h_bank")
                 for t in range(PACK):
@@ -157,17 +165,21 @@ def tile_list_tabgate_gelu_kernel(tc, tab_words, tab_scales, w1, w2_words, w2_sc
 
         def finish(g):
             u0, u1 = GROUPS[g]
-            activated = held.tile([P, (u1 - u0) * UNIT], F32, name=f"activated{g}", tag=f"shared{g + LAG}", align_bytes=64)
+            activated = held.tile([P, (u1 - u0) * UNIT], F32, name=f"activated{g}", tag=f"shared{g + REUSE_LAG}", align_bytes=64)
             nc.scalar.activation(activated[:], y_banks[g][:], ACT.Gelu_apprx_tanh, bias=bias[:])
             nc.vector.tensor_tensor(
                 result[g][:], gates[:].indirect(list_slice(u0 * UNIT, u1 * UNIT)), activated[:], ALU.mult
             )
             nc.sync.dma_start(out[:, u0 * UNIT : u1 * UNIT], result[g][:])
 
-        for g in range(len(GROUPS) + LAG):
-            if g >= LAG:
-                finish(g - LAG)
-            if g < len(GROUPS):
-                first_layer(g)
-                quantize_h(g)
-                second_layer(g)
+        units = S // UNIT
+        group_ending_at = {u1 - 1: g for g, (u0, u1) in enumerate(GROUPS)}
+        for step in range(units + FINISH_LAG):
+            if step < units:
+                first_layer(step)
+            if step in group_ending_at:
+                quantize_h(group_ending_at[step])
+            if step - SECOND_LAG in group_ending_at:
+                second_layer(group_ending_at[step - SECOND_LAG])
+            if step - FINISH_LAG in group_ending_at:
+                finish(group_ending_at[step - FINISH_LAG])

@@ -18,16 +18,22 @@ ALU = mybir.AluOpType
 
 P = 128
 PACK = 4
+HALF = P // 2
+LIST_ROWS = 16
+SCALE_ROWS = 16
+QUADRANT = 32
+
 UNIT = 128
+GROUPS = [(u, u + 2) for u in range(0, S // UNIT, 2)]
 GATHER = 512
 W1_PIECES = [(0, 256), (256, 384), (384, 512)]
-GROUPS = [(0, 2), (2, 4), (4, 6), (6, 8), (8, 10), (10, 11), (11, 12)]
 VECTOR_UNITS = (2, 4, 6)
-SECOND_LAG = 3
-FINISH_LAG = 3
+SECOND_LAG = 2
+FINISH_LAG = 4
 REUSE_LAG = 4
 H_BANKS = 5
-HALF = P // 2
+Y_BANKS = 3
+WARM_COLUMNS = ((0, 512), (0, 256))
 
 
 def tile_list_tabgate_gelu_kernel(tc, tab_words, tab_scales, w1, w2_words, w2_scales, gT, b, offs, out):
@@ -35,47 +41,47 @@ def tile_list_tabgate_gelu_kernel(tc, tab_words, tab_scales, w1, w2_words, w2_sc
     with ExitStack() as ctx:
         held = ctx.enter_context(tc.tile_pool(name="held", bufs=1))
         h_psum = ctx.enter_context(tc.psum_pool(name="h_psum", bufs=H_BANKS))
-        y_psum = ctx.enter_context(tc.psum_pool(name="y_psum", bufs=8 - H_BANKS))
+        y_psum = ctx.enter_context(tc.psum_pool(name="y_psum", bufs=Y_BANKS))
 
-        offsets = held.tile([P, S // 16], U16, name="offsets")
+        offsets = held.tile([P, S // LIST_ROWS], U16, name="offsets")
         table_words = held.tile([P, T], I32, name="table_words", align_bytes=64)
         table_scales = held.tile([P, T // 4], I32, name="table_scales", align_bytes=64)
         gates = held.tile([P, T], F32, name="gates", align_bytes=64)
         w2_codes = held.tile([P, 2 * M], U8, name="w2_codes", align_bytes=64)
-        w2_plane = held.tile([P, M // 4], I32, name="w2_plane", align_bytes=64)
+        w2_scale_tile = held.tile([P, M // 4], I32, name="w2_scale_tile", align_bytes=64)
         bias = held.tile([P, 1], F32, name="bias")
-        warm_in = held.tile([P, 1], F32, name="warm_in")
-        warm_out = held.tile([P, 1], F32, name="warm_out")
+        gelu_warm_in = held.tile([P, 1], F32, name="gelu_warm_in")
+        gelu_warm_out = held.tile([P, 1], F32, name="gelu_warm_out")
         w1_raw = [held.tile([P, PACK, c1 - c0], F32, name=f"w1_raw{c0}", align_bytes=64) for c0, c1 in W1_PIECES]
         w1_grouped = held.tile([P, PACK, P, PACK], BF16, name="w1_grouped", tag="w1_then_words", align_bytes=64)
         w1_codes = held.tile([P, H], U32, name="w1_codes", align_bytes=64)
-        w1_plane = held.tile([P, H], U8, name="w1_plane", align_bytes=64)
-        picked_words = [held.tile([P, GATHER], U32, name=f"picked_words{c}", align_bytes=64) for c in range(S // GATHER - 1)]
-        picked_plane = held.tile([P, S], U8, name="picked_plane", align_bytes=64)
+        w1_scale_tile = held.tile([P, H], U8, name="w1_scale_tile", align_bytes=64)
+        picked_words = [
+            held.tile([P, GATHER], U32, name=f"picked_words{c}", align_bytes=64) for c in range(S // GATHER - 1)
+        ]
+        picked_scales = held.tile([P, S], U8, name="picked_scales", align_bytes=64)
 
         nc.vector.memset(table_scales[:], 0)
-        nc.vector.memset(w2_plane[:], 0)
-        nc.gpsimd.memset(warm_in[:], 0.0)
-        nc.scalar.activation(warm_out[:], warm_in[:], ACT.Gelu_apprx_tanh)
-
-        w1_rows = w1.rearrange("(p j) c -> p j c", j=PACK)
-        tab_scale_rows = tab_scales[0].bitcast(I32)
-        w2_scale_rows = w2_scales[0].bitcast(I32)
+        nc.vector.memset(w2_scale_tile[:], 0)
+        nc.gpsimd.memset(gelu_warm_in[:], 0.0)
+        nc.scalar.activation(gelu_warm_out[:], gelu_warm_in[:], ACT.Gelu_apprx_tanh)
 
         def load_w1(i):
             c0, c1 = W1_PIECES[i]
-            nc.sync.dma_start(w1_raw[i][:], w1_rows[:, :, c0:c1])
+            nc.sync.dma_start(w1_raw[i][:], w1.rearrange("(p j) c -> p j c", j=PACK)[:, :, c0:c1])
+
+        def load_scale_rows(tile, rows):
+            for r in range(4):
+                nc.sync.dma_start(tile[r:P:QUADRANT, :], rows.bitcast(I32)[r:SCALE_ROWS:4, :])
 
         nc.sync.dma_start(offsets[:], offs)
         nc.sync.dma_start(w2_codes[:].bitcast(I32), w2_words[0].bitcast(I32))
         load_w1(0)
-        for r in range(4):
-            nc.sync.dma_start(table_scales[r:P:32, :], tab_scale_rows[r:16:4, :])
+        load_scale_rows(table_scales, tab_scales[0])
         nc.sync.dma_start(table_words[:], tab_words[0].rearrange("p n t -> p (n t)").bitcast(I32))
         for i in range(1, len(W1_PIECES)):
             load_w1(i)
-        for r in range(4):
-            nc.sync.dma_start(w2_plane[r:P:32, :], w2_scale_rows[r:16:4, :])
+        load_scale_rows(w2_scale_tile, w2_scales[0])
         nc.sync.dma_start(gates[:], gT)
         nc.gpsimd.dma_start(bias[:], b.rearrange("(p o) -> p o", o=1))
 
@@ -85,95 +91,110 @@ def tile_list_tabgate_gelu_kernel(tc, tab_words, tab_scales, w1, w2_words, w2_sc
                 w1_raw[i][:].rearrange("p j (m t) -> p m j t", t=PACK),
             )
 
-        nc.vector.tensor_copy(picked_plane[:], table_scales[:].bitcast(U8).indirect(offsets[:]))
-
         def list_slice(s0, s1):
-            return offsets[:, s0 // 16 : s1 // 16]
+            return offsets[:, s0 // LIST_ROWS : s1 // LIST_ROWS]
 
         def gather_words(c):
             nc.vector.tensor_copy(
                 picked_words[c][:], table_words[:].bitcast(U32).indirect(list_slice(c * GATHER, (c + 1) * GATHER))
             )
 
-        def quantize_w1(m0):
-            for t in range(PACK):
-                cols = slice(t * P + m0, t * P + m0 + HALF)
-                nc.vector.quantize_mx(
-                    out=w1_codes[:, cols].bitcast(FP8X4),
-                    scales=w1_plane[:, cols],
-                    in_=w1_grouped[:, t, m0 : m0 + HALF, :].rearrange("p m j -> p (m j)"),
-                )
+        def quantize_w1(t, m0, codes, scale_tile, c0):
+            nc.vector.quantize_mx(
+                out=codes[:, c0 : c0 + HALF].bitcast(FP8X4),
+                scales=scale_tile[:, c0 : c0 + HALF],
+                in_=w1_grouped[:, t, m0 : m0 + HALF, :].rearrange("p m j -> p (m j)"),
+            )
 
-        quantize_w1(0)
+        nc.vector.tensor_copy(picked_scales[:], table_scales[:].bitcast(U8).indirect(offsets[:]))
+        for t in range(PACK):
+            quantize_w1(t, 0, w1_codes, w1_scale_tile, t * P)
+
+        pe_warm_codes = held.tile([P, P], U32, name="pe_warm_codes", align_bytes=64)
+        pe_warm_scale_tile = held.tile([P, P], U8, name="pe_warm_scale_tile", align_bytes=64)
+        for t in range(P // HALF):
+            quantize_w1(t, 0, pe_warm_codes, pe_warm_scale_tile, t * HALF)
         gather_words(0)
+        for n0, n1 in WARM_COLUMNS:
+            bank = h_psum.tile([P, PACK, UNIT], F32, name="h_bank")
+            nc.tensor.matmul_mx(
+                out=bank[:].rearrange("p t n -> p (t n)")[:, 0 : n1 - n0],
+                lhsT=pe_warm_codes[:].bitcast(FP8X4),
+                lhsT_scale=pe_warm_scale_tile[:],
+                rhs=picked_words[0][:, n0:n1].bitcast(FP8X4),
+                rhs_scale=picked_scales[:, n0:n1],
+                start=True,
+                stop=True,
+            )
+
         gather_words(1)
-        quantize_w1(HALF)
+        for t in range(PACK):
+            quantize_w1(t, HALF, w1_codes, w1_scale_tile, t * P + HALF)
         picked_words.append(held.tile([P, GATHER], U32, name="picked_words_last", tag="w1_then_words", align_bytes=64))
         gather_words(2)
 
-        h_grouped = [held.tile([P, (u1 - u0) * UNIT, PACK], BF16, name=f"h_grouped{u0}", align_bytes=64) for u0, u1 in GROUPS]
+        widths = [(u1 - u0) * UNIT for u0, u1 in GROUPS]
+        h_grouped = [held.tile([P, w, PACK], BF16, name=f"h_grouped{g}", align_bytes=64) for g, w in enumerate(widths)]
+        h_scale_tile = [held.tile([P, w], U8, name=f"h_scale_tile{g}", align_bytes=64) for g, w in enumerate(widths)]
+        result = [held.tile([P, w], F32, name=f"result{g}", align_bytes=64) for g, w in enumerate(widths)]
         h_codes = {}
-        h_plane = [held.tile([P, (u1 - u0) * UNIT], U8, name=f"h_plane{u0}", align_bytes=64) for u0, u1 in GROUPS]
-        result = [held.tile([P, (u1 - u0) * UNIT], F32, name=f"result{u0}", align_bytes=64) for u0, u1 in GROUPS]
         y_banks = {}
+        group_of_unit = {u: g for g, (u0, u1) in enumerate(GROUPS) for u in range(u0, u1)}
+        group_ending_at = {u1 - 1: g for g, (u0, u1) in enumerate(GROUPS)}
 
         def first_layer(u):
-            g = [u0 <= u < u1 for u0, u1 in GROUPS].index(True)
-            u0 = GROUPS[g][0]
-            if True:
-                c, s0 = divmod(u * UNIT, GATHER)
-                bank = h_psum.tile([P, PACK, UNIT], F32, name="h_bank")
-                for t in range(PACK):
-                    cols = slice(t * P, (t + 1) * P)
-                    nc.tensor.matmul_mx(
-                        out=bank[:, t, :],
-                        lhsT=w1_codes[:, cols].bitcast(FP8X4),
-                        lhsT_scale=w1_plane[:, cols],
-                        rhs=picked_words[c][:, s0 : s0 + UNIT].bitcast(FP8X4),
-                        rhs_scale=picked_plane[:, u * UNIT : (u + 1) * UNIT],
-                        start=True,
-                        stop=True,
-                    )
-                dst = h_grouped[g][:, (u - u0) * UNIT : (u - u0 + 1) * UNIT, :]
-                src = bank[:].rearrange("p t n -> p n t")
-                if u in VECTOR_UNITS:
-                    nc.vector.tensor_scalar_max(dst, src, 0.0)
-                else:
-                    nc.scalar.activation(dst, src, ACT.Relu)
+            g = group_of_unit[u]
+            c, s0 = divmod(u * UNIT, GATHER)
+            bank = h_psum.tile([P, PACK, UNIT], F32, name="h_bank")
+            for t in range(PACK):
+                cols = slice(t * P, (t + 1) * P)
+                nc.tensor.matmul_mx(
+                    out=bank[:, t, :],
+                    lhsT=w1_codes[:, cols].bitcast(FP8X4),
+                    lhsT_scale=w1_scale_tile[:, cols],
+                    rhs=picked_words[c][:, s0 : s0 + UNIT].bitcast(FP8X4),
+                    rhs_scale=picked_scales[:, u * UNIT : (u + 1) * UNIT],
+                    start=True,
+                    stop=True,
+                )
+            n0 = (u - GROUPS[g][0]) * UNIT
+            interleaved = h_grouped[g][:, n0 : n0 + UNIT, :]
+            sums = bank[:].rearrange("p t n -> p n t")
+            if u in VECTOR_UNITS:
+                nc.vector.tensor_scalar_max(interleaved, sums, 0.0)
+            else:
+                nc.scalar.activation(interleaved, sums, ACT.Relu)
 
         def quantize_h(g):
-            u0, u1 = GROUPS[g]
-            h_codes[g] = held.tile([P, (u1 - u0) * UNIT], U32, name=f"h_codes{g}", tag=f"shared{g}", align_bytes=64)
+            h_codes[g] = held.tile([P, widths[g]], U32, name=f"h_codes{g}", tag=f"shared{g}", align_bytes=64)
             nc.vector.quantize_mx(
                 out=h_codes[g][:].bitcast(FP8X4),
-                scales=h_plane[g][:],
+                scales=h_scale_tile[g][:],
                 in_=h_grouped[g][:].rearrange("p n t -> p (n t)"),
             )
 
         def second_layer(g):
-            u0, u1 = GROUPS[g]
-            y_banks[g] = y_psum.tile([P, (u1 - u0) * UNIT], F32, name="y_bank")
+            y_banks[g] = y_psum.tile([P, widths[g]], F32, name="y_bank")
             nc.tensor.matmul_mx(
                 out=y_banks[g][:],
                 lhsT=w2_codes[:].bitcast(FP4X4),
-                lhsT_scale=w2_plane[:].bitcast(U8),
+                lhsT_scale=w2_scale_tile[:].bitcast(U8),
                 rhs=h_codes[g][:].bitcast(FP8X4),
-                rhs_scale=h_plane[g][:],
+                rhs_scale=h_scale_tile[g][:],
                 start=True,
                 stop=True,
             )
 
         def finish(g):
-            u0, u1 = GROUPS[g]
-            activated = held.tile([P, (u1 - u0) * UNIT], F32, name=f"activated{g}", tag=f"shared{g + REUSE_LAG}", align_bytes=64)
-            nc.scalar.activation(activated[:], y_banks[g][:], ACT.Gelu_apprx_tanh, bias=bias[:])
-            nc.vector.tensor_tensor(
-                result[g][:], gates[:].indirect(list_slice(u0 * UNIT, u1 * UNIT)), activated[:], ALU.mult
+            s0, s1 = GROUPS[g][0] * UNIT, GROUPS[g][1] * UNIT
+            activated = held.tile(
+                [P, widths[g]], F32, name=f"activated{g}", tag=f"shared{g + REUSE_LAG}", align_bytes=64
             )
-            nc.sync.dma_start(out[:, u0 * UNIT : u1 * UNIT], result[g][:])
+            nc.scalar.activation(activated[:], y_banks[g][:], ACT.Gelu_apprx_tanh, bias=bias[:])
+            nc.vector.tensor_tensor(result[g][:], gates[:].indirect(list_slice(s0, s1)), activated[:], ALU.mult)
+            nc.sync.dma_start(out[:, s0:s1], result[g][:])
 
         units = S // UNIT
-        group_ending_at = {u1 - 1: g for g, (u0, u1) in enumerate(GROUPS)}
         for step in range(units + FINISH_LAG):
             if step < units:
                 first_layer(step)

@@ -24,16 +24,20 @@ SCALE_ROWS = 16
 QUADRANT = 32
 
 UNIT = 128
-GROUPS = [(u, u + 2) for u in range(0, S // UNIT, 2)]
 GATHER = 512
-W1_PIECES = [(0, 256), (256, 384), (384, 512)]
-VECTOR_UNITS = (2, 4, 6)
-SECOND_LAG = 2
-FINISH_LAG = 4
-REUSE_LAG = 4
+GROUPS = [(0, 4), (4, 6), (6, 8), (8, 10), (10, 11), (11, 12)]
+VECTOR_UNITS = (3, 6)
+GPSIMD_GROUPS = ()
 H_BANKS = 5
 Y_BANKS = 3
-WARM_COLUMNS = ((0, 512), (0, 256))
+WORDS_TAG = {1: "w1_grouped"}
+GATES_TAG = {}
+CODES_TAG = {3: "activated0", 4: "activated2"}
+ORDER = "h0 w0 h1 w1 u0 u1 u2 u3 q0 u4 y0 u5 q1 u6 y1 u7 q2 a0 u8 y2 a1 a2 u9 m0 m1 q3 y3 u10 m2 q4 u11 q5 a3 y4 y5 m3 a4 m4 a5 m5"
+W1_PIECES = [(0, 256), (256, 384), (384, 512)]
+WORD_CHUNKS = [(0, 768), (768, 1536)]
+SHARE_LAST = True
+GROUPED_TAG = {}
 
 
 def tile_list_tabgate_gelu_kernel(tc, tab_words, tab_scales, w1, w2_words, w2_scales, gT, b, offs, out):
@@ -45,7 +49,7 @@ def tile_list_tabgate_gelu_kernel(tc, tab_words, tab_scales, w1, w2_words, w2_sc
 
         offsets = held.tile([P, S // LIST_ROWS], U16, name="offsets")
         table_words = held.tile([P, T], I32, name="table_words", align_bytes=64)
-        table_scales = held.tile([P, T // 4], I32, name="table_scales", align_bytes=64)
+        table_scales = held.tile([P, T // 4], I32, name="table_scales", tag="scales_then_codes", align_bytes=64)
         gates = held.tile([P, T], F32, name="gates", align_bytes=64)
         w2_codes = held.tile([P, 2 * M], U8, name="w2_codes", align_bytes=64)
         w2_scale_tile = held.tile([P, M // 4], I32, name="w2_scale_tile", align_bytes=64)
@@ -53,34 +57,28 @@ def tile_list_tabgate_gelu_kernel(tc, tab_words, tab_scales, w1, w2_words, w2_sc
         gelu_warm_in = held.tile([P, 1], F32, name="gelu_warm_in")
         gelu_warm_out = held.tile([P, 1], F32, name="gelu_warm_out")
         w1_raw = [held.tile([P, PACK, c1 - c0], F32, name=f"w1_raw{c0}", align_bytes=64) for c0, c1 in W1_PIECES]
-        w1_grouped = held.tile([P, PACK, P, PACK], BF16, name="w1_grouped", tag="w1_then_words", align_bytes=64)
-        w1_codes = held.tile([P, H], U32, name="w1_codes", align_bytes=64)
+        w1_grouped = held.tile([P, PACK, P, PACK], BF16, name="w1_grouped", tag="w1_grouped", align_bytes=64)
         w1_scale_tile = held.tile([P, H], U8, name="w1_scale_tile", align_bytes=64)
-        picked_words = [
-            held.tile([P, GATHER], U32, name=f"picked_words{c}", align_bytes=64) for c in range(S // GATHER - 1)
-        ]
         picked_scales = held.tile([P, S], U8, name="picked_scales", align_bytes=64)
 
-        nc.vector.memset(table_scales[:], 0)
+        nc.gpsimd.memset(table_scales[:, 0:512], 0)
+        nc.vector.memset(table_scales[:, 512:1024], 0)
         nc.vector.memset(w2_scale_tile[:], 0)
         nc.gpsimd.memset(gelu_warm_in[:], 0.0)
         nc.scalar.activation(gelu_warm_out[:], gelu_warm_in[:], ACT.Gelu_apprx_tanh)
-
-        def load_w1(i):
-            c0, c1 = W1_PIECES[i]
-            nc.sync.dma_start(w1_raw[i][:], w1.rearrange("(p j) c -> p j c", j=PACK)[:, :, c0:c1])
 
         def load_scale_rows(tile, rows):
             for r in range(4):
                 nc.sync.dma_start(tile[r:P:QUADRANT, :], rows.bitcast(I32)[r:SCALE_ROWS:4, :])
 
         nc.sync.dma_start(offsets[:], offs)
-        nc.sync.dma_start(w2_codes[:].bitcast(I32), w2_words[0].bitcast(I32))
-        load_w1(0)
+        w1_rows = w1.rearrange("(p j) c -> p j c", j=PACK)
+        nc.sync.dma_start(w1_raw[0][:], w1_rows[:, :, W1_PIECES[0][0] : W1_PIECES[0][1]])
         load_scale_rows(table_scales, tab_scales[0])
         nc.sync.dma_start(table_words[:], tab_words[0].rearrange("p n t -> p (n t)").bitcast(I32))
         for i in range(1, len(W1_PIECES)):
-            load_w1(i)
+            nc.sync.dma_start(w1_raw[i][:], w1_rows[:, :, W1_PIECES[i][0] : W1_PIECES[i][1]])
+        nc.sync.dma_start(w2_codes[:].bitcast(I32), w2_words[0].bitcast(I32))
         load_scale_rows(w2_scale_tile, w2_scales[0])
         nc.sync.dma_start(gates[:], gT)
         nc.gpsimd.dma_start(bias[:], b.rearrange("(p o) -> p o", o=1))
@@ -94,57 +92,50 @@ def tile_list_tabgate_gelu_kernel(tc, tab_words, tab_scales, w1, w2_words, w2_sc
         def list_slice(s0, s1):
             return offsets[:, s0 // LIST_ROWS : s1 // LIST_ROWS]
 
+        picked_words = {}
+
         def gather_words(c):
+            s0, s1 = WORD_CHUNKS[c]
+            picked_words[c] = held.tile([P, s1 - s0], U32, name=f"picked_words{c}", tag=WORDS_TAG.get(c, f"picked_words{c}"), align_bytes=64)
             nc.vector.tensor_copy(
-                picked_words[c][:], table_words[:].bitcast(U32).indirect(list_slice(c * GATHER, (c + 1) * GATHER))
+                picked_words[c][:], table_words[:].bitcast(U32).indirect(list_slice(s0, s1))
             )
 
-        def quantize_w1(t, m0, codes, scale_tile, c0):
-            nc.vector.quantize_mx(
-                out=codes[:, c0 : c0 + HALF].bitcast(FP8X4),
-                scales=scale_tile[:, c0 : c0 + HALF],
-                in_=w1_grouped[:, t, m0 : m0 + HALF, :].rearrange("p m j -> p (m j)"),
-            )
+        picked_gates = {}
+
+        def gather_gates(c):
+            picked_gates[c] = held.tile([P, GATHER], F32, name=f"picked_gates{c}", tag=GATES_TAG.get(c, f"picked_gates{c}"), align_bytes=64)
+            nc.vector.tensor_copy(picked_gates[c][:], gates[:].indirect(list_slice(c * GATHER, (c + 1) * GATHER)))
 
         nc.vector.tensor_copy(picked_scales[:], table_scales[:].bitcast(U8).indirect(offsets[:]))
-        for t in range(PACK):
-            quantize_w1(t, 0, w1_codes, w1_scale_tile, t * P)
+        w1_codes = held.tile([P, H], U32, name="w1_codes", tag="scales_then_codes", align_bytes=64)
 
-        pe_warm_codes = held.tile([P, P], U32, name="pe_warm_codes", align_bytes=64)
-        pe_warm_scale_tile = held.tile([P, P], U8, name="pe_warm_scale_tile", align_bytes=64)
-        for t in range(P // HALF):
-            quantize_w1(t, 0, pe_warm_codes, pe_warm_scale_tile, t * HALF)
-        gather_words(0)
-        for n0, n1 in WARM_COLUMNS:
-            bank = h_psum.tile([P, PACK, UNIT], F32, name="h_bank")
-            nc.tensor.matmul_mx(
-                out=bank[:].rearrange("p t n -> p (t n)")[:, 0 : n1 - n0],
-                lhsT=pe_warm_codes[:].bitcast(FP8X4),
-                lhsT_scale=pe_warm_scale_tile[:],
-                rhs=picked_words[0][:, n0:n1].bitcast(FP8X4),
-                rhs_scale=picked_scales[:, n0:n1],
-                start=True,
-                stop=True,
-            )
-
-        gather_words(1)
-        for t in range(PACK):
-            quantize_w1(t, HALF, w1_codes, w1_scale_tile, t * P + HALF)
-        picked_words.append(held.tile([P, GATHER], U32, name="picked_words_last", tag="w1_then_words", align_bytes=64))
-        gather_words(2)
+        def quantize_w1(half):
+            m0 = half * HALF
+            for t in range(PACK):
+                c0 = t * P + m0
+                nc.vector.quantize_mx(
+                    out=w1_codes[:, c0 : c0 + HALF].bitcast(FP8X4),
+                    scales=w1_scale_tile[:, c0 : c0 + HALF],
+                    in_=w1_grouped[:, t, m0 : m0 + HALF, :].rearrange("p m j -> p (m j)"),
+                )
 
         widths = [(u1 - u0) * UNIT for u0, u1 in GROUPS]
-        h_grouped = [held.tile([P, w, PACK], BF16, name=f"h_grouped{g}", align_bytes=64) for g, w in enumerate(widths)]
+        h_grouped = {}
         h_scale_tile = [held.tile([P, w], U8, name=f"h_scale_tile{g}", align_bytes=64) for g, w in enumerate(widths)]
         result = [held.tile([P, w], F32, name=f"result{g}", align_bytes=64) for g, w in enumerate(widths)]
         h_codes = {}
+        last_codes = []
         y_banks = {}
+        activated = {}
         group_of_unit = {u: g for g, (u0, u1) in enumerate(GROUPS) for u in range(u0, u1)}
-        group_ending_at = {u1 - 1: g for g, (u0, u1) in enumerate(GROUPS)}
 
         def first_layer(u):
             g = group_of_unit[u]
-            c, s0 = divmod(u * UNIT, GATHER)
+            if g not in h_grouped:
+                h_grouped[g] = held.tile([P, widths[g], PACK], BF16, name=f"h_grouped{g}", tag=GROUPED_TAG.get(g, f"h_grouped{g}"), align_bytes=64)
+            c = max(i for i, chunk in enumerate(WORD_CHUNKS) if chunk[0] <= u * UNIT)
+            s0 = u * UNIT - WORD_CHUNKS[c][0]
             bank = h_psum.tile([P, PACK, UNIT], F32, name="h_bank")
             for t in range(PACK):
                 cols = slice(t * P, (t + 1) * P)
@@ -166,9 +157,15 @@ def tile_list_tabgate_gelu_kernel(tc, tab_words, tab_scales, w1, w2_words, w2_sc
                 nc.scalar.activation(interleaved, sums, ACT.Relu)
 
         def quantize_h(g):
-            h_codes[g] = held.tile([P, widths[g]], U32, name=f"h_codes{g}", tag=f"shared{g}", align_bytes=64)
+            if g == len(GROUPS) - 1 and SHARE_LAST:
+                h_codes[g] = last_codes[0][:, widths[g - 1] : widths[g - 1] + widths[g]]
+            elif g == len(GROUPS) - 2 and SHARE_LAST:
+                last_codes.append(held.tile([P, widths[g] + widths[g + 1]], U32, name=f"h_codes{g}", tag=CODES_TAG.get(g, f"h_codes{g}"), align_bytes=64))
+                h_codes[g] = last_codes[0][:, 0 : widths[g]]
+            else:
+                h_codes[g] = held.tile([P, widths[g]], U32, name=f"h_codes{g}", tag=CODES_TAG.get(g, f"h_codes{g}"), align_bytes=64)[:]
             nc.vector.quantize_mx(
-                out=h_codes[g][:].bitcast(FP8X4),
+                out=h_codes[g].bitcast(FP8X4),
                 scales=h_scale_tile[g][:],
                 in_=h_grouped[g][:].rearrange("p n t -> p (n t)"),
             )
@@ -179,28 +176,27 @@ def tile_list_tabgate_gelu_kernel(tc, tab_words, tab_scales, w1, w2_words, w2_sc
                 out=y_banks[g][:],
                 lhsT=w2_codes[:].bitcast(FP4X4),
                 lhsT_scale=w2_scale_tile[:].bitcast(U8),
-                rhs=h_codes[g][:].bitcast(FP8X4),
+                rhs=h_codes[g].bitcast(FP8X4),
                 rhs_scale=h_scale_tile[g][:],
                 start=True,
                 stop=True,
             )
 
-        def finish(g):
+        def gelu(g):
+            activated[g] = held.tile([P, widths[g]], F32, name=f"activated{g}", tag=f"activated{g}", align_bytes=64)
+            nc.scalar.activation(activated[g][:], y_banks[g][:], ACT.Gelu_apprx_tanh, bias=bias[:])
+
+        def gate(g):
             s0, s1 = GROUPS[g][0] * UNIT, GROUPS[g][1] * UNIT
-            activated = held.tile(
-                [P, widths[g]], F32, name=f"activated{g}", tag=f"shared{g + REUSE_LAG}", align_bytes=64
-            )
-            nc.scalar.activation(activated[:], y_banks[g][:], ACT.Gelu_apprx_tanh, bias=bias[:])
-            nc.vector.tensor_tensor(result[g][:], gates[:].indirect(list_slice(s0, s1)), activated[:], ALU.mult)
+            c, n0 = divmod(s0, GATHER)
+            if c not in picked_gates:
+                nc.vector.tensor_tensor(result[g][:], gates[:].indirect(list_slice(s0, s1)), activated[g][:], ALU.mult)
+            elif g in GPSIMD_GROUPS:
+                nc.gpsimd.tensor_tensor(result[g][:], picked_gates[c][:, n0 : n0 + s1 - s0], activated[g][:], ALU.mult)
+            else:
+                nc.vector.tensor_tensor(result[g][:], picked_gates[c][:, n0 : n0 + s1 - s0], activated[g][:], ALU.mult)
             nc.sync.dma_start(out[:, s0:s1], result[g][:])
 
-        units = S // UNIT
-        for step in range(units + FINISH_LAG):
-            if step < units:
-                first_layer(step)
-            if step in group_ending_at:
-                quantize_h(group_ending_at[step])
-            if step - SECOND_LAG in group_ending_at:
-                second_layer(group_ending_at[step - SECOND_LAG])
-            if step - FINISH_LAG in group_ending_at:
-                finish(group_ending_at[step - FINISH_LAG])
+        steps = {"h": quantize_w1, "w": gather_words, "G": gather_gates, "u": first_layer, "q": quantize_h, "y": second_layer, "a": gelu, "m": gate}
+        for step in ORDER.split():
+            steps[step[0]](int(step[1:]))

@@ -25,18 +25,18 @@ QUADRANT = 32
 
 UNIT = 128
 GATHER = 512
-GROUPS = [(0, 4), (4, 6), (6, 8), (8, 10), (10, 11), (11, 12)]
-VECTOR_UNITS = (3, 6)
+GROUPS = [(u, u + 2) for u in range(0, 12, 2)]
+VECTOR_UNITS = (2, 4, 7)
 GPSIMD_GROUPS = ()
 H_BANKS = 5
 Y_BANKS = 3
 WORDS_TAG = {1: "w1_grouped"}
 GATES_TAG = {}
-CODES_TAG = {3: "activated0", 4: "activated2"}
-ORDER = "h0 w0 h1 w1 u0 u1 u2 u3 q0 u4 y0 u5 q1 u6 y1 u7 q2 a0 u8 y2 a1 a2 u9 m0 m1 q3 y3 u10 m2 q4 u11 q5 a3 y4 y5 m3 a4 m4 a5 m5"
+CODES_TAG = {3: "activated0", 4: "activated1", 5: "activated2"}
+ORDER = "h0 w0 h1 w1 u0 u1 q0 u2 y0 u3 q1 a0 u4 m0 y1 u5 q2 a1 u6 m1 y2 u7 q3 a2 u8 m2 y3 u9 q4 a3 u10 m3 y4 u11 q5 a4 m4 y5 a5 m5"
 W1_PIECES = [(0, 256), (256, 384), (384, 512)]
 WORD_CHUNKS = [(0, 768), (768, 1536)]
-SHARE_LAST = True
+SHARE_LAST = False
 GROUPED_TAG = {}
 
 

@@ -24,20 +24,17 @@ SCALE_ROWS = 16
 QUADRANT = 32
 
 UNIT = 128
-GATHER = 512
-GROUPS = [(u, u + 2) for u in range(0, 12, 2)]
-VECTOR_UNITS = (2, 4, 7)
-GPSIMD_GROUPS = ()
+GROUP_UNITS = 2
+GROUP = GROUP_UNITS * UNIT
+GATHER = 768
+W1_PIECES = [(0, 256), (256, 384), (384, 512)]
+VECTOR_GROUPS = range(1, 4)
+SECOND_LAG = 1
+GELU_LAG = 2
+GATE_LAG = 3
+REUSE_LAG = 3
 H_BANKS = 5
 Y_BANKS = 3
-WORDS_TAG = {1: "w1_grouped"}
-GATES_TAG = {}
-CODES_TAG = {3: "activated0", 4: "activated1", 5: "activated2"}
-ORDER = "h0 w0 h1 w1 u0 u1 q0 u2 y0 u3 q1 a0 u4 m0 y1 u5 q2 a1 u6 m1 y2 u7 q3 a2 u8 m2 y3 u9 q4 a3 u10 m3 y4 u11 q5 a4 m4 y5 a5 m5"
-W1_PIECES = [(0, 256), (256, 384), (384, 512)]
-WORD_CHUNKS = [(0, 768), (768, 1536)]
-SHARE_LAST = False
-GROUPED_TAG = {}
 
 
 def tile_list_tabgate_gelu_kernel(tc, tab_words, tab_scales, w1, w2_words, w2_scales, gT, b, offs, out):
@@ -57,27 +54,30 @@ def tile_list_tabgate_gelu_kernel(tc, tab_words, tab_scales, w1, w2_words, w2_sc
         gelu_warm_in = held.tile([P, 1], F32, name="gelu_warm_in")
         gelu_warm_out = held.tile([P, 1], F32, name="gelu_warm_out")
         w1_raw = [held.tile([P, PACK, c1 - c0], F32, name=f"w1_raw{c0}", align_bytes=64) for c0, c1 in W1_PIECES]
-        w1_grouped = held.tile([P, PACK, P, PACK], BF16, name="w1_grouped", tag="w1_grouped", align_bytes=64)
+        w1_grouped = held.tile([P, PACK, P, PACK], BF16, name="w1_grouped", tag="w1_then_words", align_bytes=64)
         w1_scale_tile = held.tile([P, H], U8, name="w1_scale_tile", align_bytes=64)
         picked_scales = held.tile([P, S], U8, name="picked_scales", align_bytes=64)
 
-        nc.gpsimd.memset(table_scales[:, 0:512], 0)
-        nc.vector.memset(table_scales[:, 512:1024], 0)
+        nc.gpsimd.memset(table_scales[:, 0 : T // 8], 0)
+        nc.vector.memset(table_scales[:, T // 8 : T // 4], 0)
         nc.vector.memset(w2_scale_tile[:], 0)
         nc.gpsimd.memset(gelu_warm_in[:], 0.0)
         nc.scalar.activation(gelu_warm_out[:], gelu_warm_in[:], ACT.Gelu_apprx_tanh)
+
+        def load_w1(i):
+            c0, c1 = W1_PIECES[i]
+            nc.sync.dma_start(w1_raw[i][:], w1.rearrange("(p j) c -> p j c", j=PACK)[:, :, c0:c1])
 
         def load_scale_rows(tile, rows):
             for r in range(4):
                 nc.sync.dma_start(tile[r:P:QUADRANT, :], rows.bitcast(I32)[r:SCALE_ROWS:4, :])
 
         nc.sync.dma_start(offsets[:], offs)
-        w1_rows = w1.rearrange("(p j) c -> p j c", j=PACK)
-        nc.sync.dma_start(w1_raw[0][:], w1_rows[:, :, W1_PIECES[0][0] : W1_PIECES[0][1]])
+        load_w1(0)
         load_scale_rows(table_scales, tab_scales[0])
         nc.sync.dma_start(table_words[:], tab_words[0].rearrange("p n t -> p (n t)").bitcast(I32))
         for i in range(1, len(W1_PIECES)):
-            nc.sync.dma_start(w1_raw[i][:], w1_rows[:, :, W1_PIECES[i][0] : W1_PIECES[i][1]])
+            load_w1(i)
         nc.sync.dma_start(w2_codes[:].bitcast(I32), w2_words[0].bitcast(I32))
         load_scale_rows(w2_scale_tile, w2_scales[0])
         nc.sync.dma_start(gates[:], gT)
@@ -92,50 +92,43 @@ def tile_list_tabgate_gelu_kernel(tc, tab_words, tab_scales, w1, w2_words, w2_sc
         def list_slice(s0, s1):
             return offsets[:, s0 // LIST_ROWS : s1 // LIST_ROWS]
 
-        picked_words = {}
-
-        def gather_words(c):
-            s0, s1 = WORD_CHUNKS[c]
-            picked_words[c] = held.tile([P, s1 - s0], U32, name=f"picked_words{c}", tag=WORDS_TAG.get(c, f"picked_words{c}"), align_bytes=64)
+        def gather_words(c, tag):
+            words = held.tile([P, GATHER], U32, name=f"picked_words{c}", tag=tag, align_bytes=64)
             nc.vector.tensor_copy(
-                picked_words[c][:], table_words[:].bitcast(U32).indirect(list_slice(s0, s1))
+                words[:], table_words[:].bitcast(U32).indirect(list_slice(c * GATHER, (c + 1) * GATHER))
             )
-
-        picked_gates = {}
-
-        def gather_gates(c):
-            picked_gates[c] = held.tile([P, GATHER], F32, name=f"picked_gates{c}", tag=GATES_TAG.get(c, f"picked_gates{c}"), align_bytes=64)
-            nc.vector.tensor_copy(picked_gates[c][:], gates[:].indirect(list_slice(c * GATHER, (c + 1) * GATHER)))
+            return words
 
         nc.vector.tensor_copy(picked_scales[:], table_scales[:].bitcast(U8).indirect(offsets[:]))
         w1_codes = held.tile([P, H], U32, name="w1_codes", tag="scales_then_codes", align_bytes=64)
 
-        def quantize_w1(half):
-            m0 = half * HALF
+        def quantize_w1(m0):
             for t in range(PACK):
-                c0 = t * P + m0
+                cols = slice(t * P + m0, t * P + m0 + HALF)
                 nc.vector.quantize_mx(
-                    out=w1_codes[:, c0 : c0 + HALF].bitcast(FP8X4),
-                    scales=w1_scale_tile[:, c0 : c0 + HALF],
+                    out=w1_codes[:, cols].bitcast(FP8X4),
+                    scales=w1_scale_tile[:, cols],
                     in_=w1_grouped[:, t, m0 : m0 + HALF, :].rearrange("p m j -> p (m j)"),
                 )
 
-        widths = [(u1 - u0) * UNIT for u0, u1 in GROUPS]
+        quantize_w1(0)
+        picked_words = [gather_words(0, "picked_words0")]
+        quantize_w1(HALF)
+        picked_words.append(gather_words(1, "w1_then_words"))
+
+        groups = S // GROUP
+        h_scale_tile = [held.tile([P, GROUP], U8, name=f"h_scale_tile{g}", align_bytes=64) for g in range(groups)]
+        result = [held.tile([P, GROUP], F32, name=f"result{g}", align_bytes=64) for g in range(groups)]
         h_grouped = {}
-        h_scale_tile = [held.tile([P, w], U8, name=f"h_scale_tile{g}", align_bytes=64) for g, w in enumerate(widths)]
-        result = [held.tile([P, w], F32, name=f"result{g}", align_bytes=64) for g, w in enumerate(widths)]
         h_codes = {}
-        last_codes = []
         y_banks = {}
         activated = {}
-        group_of_unit = {u: g for g, (u0, u1) in enumerate(GROUPS) for u in range(u0, u1)}
 
         def first_layer(u):
-            g = group_of_unit[u]
-            if g not in h_grouped:
-                h_grouped[g] = held.tile([P, widths[g], PACK], BF16, name=f"h_grouped{g}", tag=GROUPED_TAG.get(g, f"h_grouped{g}"), align_bytes=64)
-            c = max(i for i, chunk in enumerate(WORD_CHUNKS) if chunk[0] <= u * UNIT)
-            s0 = u * UNIT - WORD_CHUNKS[c][0]
+            g, place = divmod(u, GROUP_UNITS)
+            if place == 0:
+                h_grouped[g] = held.tile([P, GROUP, PACK], BF16, name=f"h_grouped{g}", align_bytes=64)
+            c, s0 = divmod(u * UNIT, GATHER)
             bank = h_psum.tile([P, PACK, UNIT], F32, name="h_bank")
             for t in range(PACK):
                 cols = slice(t * P, (t + 1) * P)
@@ -148,55 +141,49 @@ def tile_list_tabgate_gelu_kernel(tc, tab_words, tab_scales, w1, w2_words, w2_sc
                     start=True,
                     stop=True,
                 )
-            n0 = (u - GROUPS[g][0]) * UNIT
-            interleaved = h_grouped[g][:, n0 : n0 + UNIT, :]
+            interleaved = h_grouped[g][:, place * UNIT : (place + 1) * UNIT, :]
             sums = bank[:].rearrange("p t n -> p n t")
-            if u in VECTOR_UNITS:
+            if place == 0 and g in VECTOR_GROUPS:
                 nc.vector.tensor_scalar_max(interleaved, sums, 0.0)
             else:
                 nc.scalar.activation(interleaved, sums, ACT.Relu)
 
         def quantize_h(g):
-            if g == len(GROUPS) - 1 and SHARE_LAST:
-                h_codes[g] = last_codes[0][:, widths[g - 1] : widths[g - 1] + widths[g]]
-            elif g == len(GROUPS) - 2 and SHARE_LAST:
-                last_codes.append(held.tile([P, widths[g] + widths[g + 1]], U32, name=f"h_codes{g}", tag=CODES_TAG.get(g, f"h_codes{g}"), align_bytes=64))
-                h_codes[g] = last_codes[0][:, 0 : widths[g]]
-            else:
-                h_codes[g] = held.tile([P, widths[g]], U32, name=f"h_codes{g}", tag=CODES_TAG.get(g, f"h_codes{g}"), align_bytes=64)[:]
+            tag = f"activated{g - REUSE_LAG}" if g >= REUSE_LAG else f"h_codes{g}"
+            h_codes[g] = held.tile([P, GROUP], U32, name=f"h_codes{g}", tag=tag, align_bytes=64)
             nc.vector.quantize_mx(
-                out=h_codes[g].bitcast(FP8X4),
+                out=h_codes[g][:].bitcast(FP8X4),
                 scales=h_scale_tile[g][:],
                 in_=h_grouped[g][:].rearrange("p n t -> p (n t)"),
             )
 
         def second_layer(g):
-            y_banks[g] = y_psum.tile([P, widths[g]], F32, name="y_bank")
+            y_banks[g] = y_psum.tile([P, GROUP], F32, name="y_bank")
             nc.tensor.matmul_mx(
                 out=y_banks[g][:],
                 lhsT=w2_codes[:].bitcast(FP4X4),
                 lhsT_scale=w2_scale_tile[:].bitcast(U8),
-                rhs=h_codes[g].bitcast(FP8X4),
+                rhs=h_codes[g][:].bitcast(FP8X4),
                 rhs_scale=h_scale_tile[g][:],
                 start=True,
                 stop=True,
             )
 
         def gelu(g):
-            activated[g] = held.tile([P, widths[g]], F32, name=f"activated{g}", tag=f"activated{g}", align_bytes=64)
+            activated[g] = held.tile([P, GROUP], F32, name=f"activated{g}", tag=f"activated{g}", align_bytes=64)
             nc.scalar.activation(activated[g][:], y_banks[g][:], ACT.Gelu_apprx_tanh, bias=bias[:])
 
-        def gate(g):
-            s0, s1 = GROUPS[g][0] * UNIT, GROUPS[g][1] * UNIT
-            c, n0 = divmod(s0, GATHER)
-            if c not in picked_gates:
-                nc.vector.tensor_tensor(result[g][:], gates[:].indirect(list_slice(s0, s1)), activated[g][:], ALU.mult)
-            elif g in GPSIMD_GROUPS:
-                nc.gpsimd.tensor_tensor(result[g][:], picked_gates[c][:, n0 : n0 + s1 - s0], activated[g][:], ALU.mult)
-            else:
-                nc.vector.tensor_tensor(result[g][:], picked_gates[c][:, n0 : n0 + s1 - s0], activated[g][:], ALU.mult)
+        def gate_and_store(g):
+            s0, s1 = g * GROUP, (g + 1) * GROUP
+            nc.vector.tensor_tensor(result[g][:], gates[:].indirect(list_slice(s0, s1)), activated[g][:], ALU.mult)
             nc.sync.dma_start(out[:, s0:s1], result[g][:])
 
-        steps = {"h": quantize_w1, "w": gather_words, "G": gather_gates, "u": first_layer, "q": quantize_h, "y": second_layer, "a": gelu, "m": gate}
-        for step in ORDER.split():
-            steps[step[0]](int(step[1:]))
+        units = S // UNIT
+        group_ending_at = {(g + 1) * GROUP_UNITS - 1: g for g in range(groups)}
+        stages = ((gate_and_store, GATE_LAG), (quantize_h, 0), (second_layer, SECOND_LAG), (gelu, GELU_LAG))
+        for step in range(units + GATE_LAG):
+            if step < units:
+                first_layer(step)
+            for stage, lag in stages:
+                if step - lag in group_ending_at:
+                    stage(group_ending_at[step - lag])

@@ -26,13 +26,17 @@ QUADRANT = 32
 UNIT = 128
 GROUP_UNITS = 2
 GROUP = GROUP_UNITS * UNIT
-GATHER = 768
-W1_PIECES = [(0, 256), (256, 384), (384, 512)]
+WORD_GATHERS = [(0, 1024), (1024, 1536)]
+WORDS_AHEAD = 512
+W1_PIECES = [(0, 128), (128, 256), (256, 384), (384, 512)]
 VECTOR_GROUPS = range(1, 4)
 SECOND_LAG = 1
 GELU_LAG = 2
 GATE_LAG = 3
 REUSE_LAG = 3
+WARM_M = 32
+WARM_N = 512
+WARM_PASSES = 5
 H_BANKS = 5
 Y_BANKS = 3
 
@@ -46,7 +50,7 @@ def tile_list_tabgate_gelu_kernel(tc, tab_words, tab_scales, w1, w2_words, w2_sc
 
         offsets = held.tile([P, S // LIST_ROWS], U16, name="offsets")
         table_words = held.tile([P, T], I32, name="table_words", align_bytes=64)
-        table_scales = held.tile([P, T // 4], I32, name="table_scales", tag="scales_then_codes", align_bytes=64)
+        table_scales = held.tile([P, T // 4], I32, name="table_scales", align_bytes=64)
         gates = held.tile([P, T], F32, name="gates", align_bytes=64)
         w2_codes = held.tile([P, 2 * M], U8, name="w2_codes", align_bytes=64)
         w2_scale_tile = held.tile([P, M // 4], I32, name="w2_scale_tile", align_bytes=64)
@@ -73,15 +77,29 @@ def tile_list_tabgate_gelu_kernel(tc, tab_words, tab_scales, w1, w2_words, w2_sc
                 nc.sync.dma_start(tile[r:P:QUADRANT, :], rows.bitcast(I32)[r:SCALE_ROWS:4, :])
 
         nc.sync.dma_start(offsets[:], offs)
-        load_w1(0)
+        words_in_hbm = tab_words[0].rearrange("p n t -> p (n t)").bitcast(I32)
+        nc.sync.dma_start(table_words[:, 0:WORDS_AHEAD], words_in_hbm[:, 0:WORDS_AHEAD])
         load_scale_rows(table_scales, tab_scales[0])
-        nc.sync.dma_start(table_words[:], tab_words[0].rearrange("p n t -> p (n t)").bitcast(I32))
-        for i in range(1, len(W1_PIECES)):
+        nc.sync.dma_start(table_words[:, WORDS_AHEAD:T], words_in_hbm[:, WORDS_AHEAD:T])
+        for i in range(len(W1_PIECES)):
             load_w1(i)
-        nc.sync.dma_start(w2_codes[:].bitcast(I32), w2_words[0].bitcast(I32))
         load_scale_rows(w2_scale_tile, w2_scales[0])
         nc.sync.dma_start(gates[:], gT)
+        nc.gpsimd.dma_start(w2_codes[:].bitcast(I32), w2_words[0].bitcast(I32))
         nc.gpsimd.dma_start(bias[:], b.rearrange("(p o) -> p o", o=1))
+
+        warm_bank = y_psum.tile([P, WARM_N], F32, name="y_bank")
+        warm_cols = slice(T - WARM_N, T)
+        for repeat in range(WARM_PASSES):
+            nc.tensor.matmul_mx(
+                out=warm_bank[0:WARM_M, :],
+                lhsT=table_words[:, T - 64 : T - 64 + WARM_M].bitcast(FP8X4),
+                lhsT_scale=table_scales[:].bitcast(U8)[:, T - 64 : T - 64 + WARM_M],
+                rhs=table_words[:, warm_cols].bitcast(FP8X4),
+                rhs_scale=table_scales[:].bitcast(U8)[:, warm_cols],
+                start=True,
+                stop=True,
+            )
 
         for i, (c0, c1) in enumerate(W1_PIECES):
             nc.scalar.copy(
@@ -93,14 +111,13 @@ def tile_list_tabgate_gelu_kernel(tc, tab_words, tab_scales, w1, w2_words, w2_sc
             return offsets[:, s0 // LIST_ROWS : s1 // LIST_ROWS]
 
         def gather_words(c, tag):
-            words = held.tile([P, GATHER], U32, name=f"picked_words{c}", tag=tag, align_bytes=64)
-            nc.vector.tensor_copy(
-                words[:], table_words[:].bitcast(U32).indirect(list_slice(c * GATHER, (c + 1) * GATHER))
-            )
+            s0, s1 = WORD_GATHERS[c]
+            words = held.tile([P, s1 - s0], U32, name=f"picked_words{c}", tag=tag, align_bytes=64)
+            nc.vector.tensor_copy(words[:], table_words[:].bitcast(U32).indirect(list_slice(s0, s1)))
             return words
 
         nc.vector.tensor_copy(picked_scales[:], table_scales[:].bitcast(U8).indirect(offsets[:]))
-        w1_codes = held.tile([P, H], U32, name="w1_codes", tag="scales_then_codes", align_bytes=64)
+        w1_codes = held.tile([P, H], U32, name="w1_codes", align_bytes=64)
 
         def quantize_w1(m0):
             for t in range(PACK):
@@ -111,8 +128,8 @@ def tile_list_tabgate_gelu_kernel(tc, tab_words, tab_scales, w1, w2_words, w2_sc
                     in_=w1_grouped[:, t, m0 : m0 + HALF, :].rearrange("p m j -> p (m j)"),
                 )
 
-        quantize_w1(0)
         picked_words = [gather_words(0, "picked_words0")]
+        quantize_w1(0)
         quantize_w1(HALF)
         picked_words.append(gather_words(1, "w1_then_words"))
 
@@ -128,7 +145,8 @@ def tile_list_tabgate_gelu_kernel(tc, tab_words, tab_scales, w1, w2_words, w2_sc
             g, place = divmod(u, GROUP_UNITS)
             if place == 0:
                 h_grouped[g] = held.tile([P, GROUP, PACK], BF16, name=f"h_grouped{g}", align_bytes=64)
-            c, s0 = divmod(u * UNIT, GATHER)
+            c = 0 if u * UNIT < WORD_GATHERS[0][1] else 1
+            s0 = u * UNIT - WORD_GATHERS[c][0]
             bank = h_psum.tile([P, PACK, UNIT], F32, name="h_bank")
             for t in range(PACK):
                 cols = slice(t * P, (t + 1) * P)

@@ -28,7 +28,8 @@ GROUP_UNITS = 2
 GROUP = GROUP_UNITS * UNIT
 WORD_GATHERS = [(0, 1024), (1024, 1536)]
 WORDS_AHEAD = 512
-W1_PIECES = [(0, 128), (128, 256), (256, 384), (384, 512)]
+W1_VECTOR_FROM = 352
+W1_PIECES = [(0, 256), (256, 512)]
 VECTOR_GROUPS = range(1, 4)
 SECOND_LAG = 1
 GELU_LAG = 2
@@ -101,11 +102,15 @@ def tile_list_tabgate_gelu_kernel(tc, tab_words, tab_scales, w1, w2_words, w2_sc
                 stop=True,
             )
 
-        for i, (c0, c1) in enumerate(W1_PIECES):
-            nc.scalar.copy(
+        def regroup_w1(copy, i, c0, c1):
+            first = W1_PIECES[i][0]
+            copy(
                 w1_grouped[:, :, c0 // PACK : c1 // PACK, :].rearrange("p t m j -> p m j t"),
-                w1_raw[i][:].rearrange("p j (m t) -> p m j t", t=PACK),
+                w1_raw[i][:, :, c0 - first : c1 - first].rearrange("p j (m t) -> p m j t", t=PACK),
             )
+
+        for i, (c0, c1) in enumerate(W1_PIECES):
+            regroup_w1(nc.scalar.copy, i, c0, min(c1, W1_VECTOR_FROM))
 
         def list_slice(s0, s1):
             return offsets[:, s0 // LIST_ROWS : s1 // LIST_ROWS]
@@ -130,6 +135,7 @@ def tile_list_tabgate_gelu_kernel(tc, tab_words, tab_scales, w1, w2_words, w2_sc
 
         picked_words = [gather_words(0, "picked_words0")]
         quantize_w1(0)
+        regroup_w1(nc.vector.tensor_copy, len(W1_PIECES) - 1, W1_VECTOR_FROM, H)
         quantize_w1(HALF)
         picked_words.append(gather_words(1, "w1_then_words"))
 

@@ -27,7 +27,7 @@ UNIT = 128
 GROUP_UNITS = 2
 GROUP = GROUP_UNITS * UNIT
 WORD_GATHERS = [(0, 1024), (1024, 1536)]
-WORDS_AHEAD = 512
+WORDS_AHEAD = 448
 W1_VECTOR_FROM = 352
 W1_PIECES = [(0, 256), (256, 512)]
 VECTOR_GROUPS = range(1, 4)
@@ -55,16 +55,14 @@ def tile_list_tabgate_gelu_kernel(tc, tab_words, tab_scales, w1, w2_words, w2_sc
         gates = held.tile([P, T], F32, name="gates", align_bytes=64)
         w2_codes = held.tile([P, 2 * M], U8, name="w2_codes", align_bytes=64)
         w2_scale_tile = held.tile([P, M // 4], I32, name="w2_scale_tile", align_bytes=64)
-        bias = held.tile([P, 1], F32, name="bias")
-        gelu_warm_in = held.tile([P, 1], F32, name="gelu_warm_in")
+        gelu_warm_in = held.tile([P, 1], F32, name="gelu_warm_in", tag="warm_then_bias")
         gelu_warm_out = held.tile([P, 1], F32, name="gelu_warm_out")
         w1_raw = [held.tile([P, PACK, c1 - c0], F32, name=f"w1_raw{c0}", align_bytes=64) for c0, c1 in W1_PIECES]
         w1_grouped = held.tile([P, PACK, P, PACK], BF16, name="w1_grouped", tag="w1_then_words", align_bytes=64)
         w1_scale_tile = held.tile([P, H], U8, name="w1_scale_tile", align_bytes=64)
         picked_scales = held.tile([P, S], U8, name="picked_scales", align_bytes=64)
 
-        nc.gpsimd.memset(table_scales[:, 0 : T // 8], 0)
-        nc.vector.memset(table_scales[:, T // 8 : T // 4], 0)
+        nc.vector.memset(table_scales[:], 0)
         nc.vector.memset(w2_scale_tile[:], 0)
         nc.gpsimd.memset(gelu_warm_in[:], 0.0)
         nc.scalar.activation(gelu_warm_out[:], gelu_warm_in[:], ACT.Gelu_apprx_tanh)
@@ -78,6 +76,7 @@ def tile_list_tabgate_gelu_kernel(tc, tab_words, tab_scales, w1, w2_words, w2_sc
                 nc.sync.dma_start(tile[r:P:QUADRANT, :], rows.bitcast(I32)[r:SCALE_ROWS:4, :])
 
         nc.sync.dma_start(offsets[:], offs)
+        nc.sync.dma_start(w2_codes[:].bitcast(I32), w2_words[0].bitcast(I32))
         words_in_hbm = tab_words[0].rearrange("p n t -> p (n t)").bitcast(I32)
         nc.sync.dma_start(table_words[:, 0:WORDS_AHEAD], words_in_hbm[:, 0:WORDS_AHEAD])
         load_scale_rows(table_scales, tab_scales[0])
@@ -86,7 +85,7 @@ def tile_list_tabgate_gelu_kernel(tc, tab_words, tab_scales, w1, w2_words, w2_sc
             load_w1(i)
         load_scale_rows(w2_scale_tile, w2_scales[0])
         nc.sync.dma_start(gates[:], gT)
-        nc.gpsimd.dma_start(w2_codes[:].bitcast(I32), w2_words[0].bitcast(I32))
+        bias = held.tile([P, 1], F32, name="bias", tag="warm_then_bias")
         nc.gpsimd.dma_start(bias[:], b.rearrange("(p o) -> p o", o=1))
 
         warm_bank = y_psum.tile([P, WARM_N], F32, name="y_bank")

@@ -28,18 +28,19 @@ GROUP_UNITS = 2
 GROUP = GROUP_UNITS * UNIT
 WORD_GATHERS = [(0, 1024), (1024, 1536)]
 WORDS_AHEAD = 448
-W1_VECTOR_FROM = 352
-W1_PIECES = [(0, 256), (256, 512)]
+W1_PIECES = [(0, H // 2), (H // 2, H)]
+W1_VECTOR_FROM = 384
 VECTOR_GROUPS = range(1, 4)
 SECOND_LAG = 1
 GELU_LAG = 2
 GATE_LAG = 3
 REUSE_LAG = 3
+H_BANKS = 6
+Y_BANKS = 2
 WARM_M = 32
 WARM_N = 512
 WARM_PASSES = 5
-H_BANKS = 5
-Y_BANKS = 3
+SCALE_ALIGN = 64
 
 
 def tile_list_tabgate_gelu_kernel(tc, tab_words, tab_scales, w1, w2_words, w2_scales, gT, b, offs, out):
@@ -55,14 +56,16 @@ def tile_list_tabgate_gelu_kernel(tc, tab_words, tab_scales, w1, w2_words, w2_sc
         gates = held.tile([P, T], F32, name="gates", align_bytes=64)
         w2_codes = held.tile([P, 2 * M], U8, name="w2_codes", align_bytes=64)
         w2_scale_tile = held.tile([P, M // 4], I32, name="w2_scale_tile", align_bytes=64)
-        gelu_warm_in = held.tile([P, 1], F32, name="gelu_warm_in", tag="warm_then_bias")
+        bias = held.tile([P, 1], F32, name="bias")
+        gelu_warm_in = held.tile([P, 1], F32, name="gelu_warm_in")
         gelu_warm_out = held.tile([P, 1], F32, name="gelu_warm_out")
         w1_raw = [held.tile([P, PACK, c1 - c0], F32, name=f"w1_raw{c0}", align_bytes=64) for c0, c1 in W1_PIECES]
         w1_grouped = held.tile([P, PACK, P, PACK], BF16, name="w1_grouped", tag="w1_then_words", align_bytes=64)
         w1_scale_tile = held.tile([P, H], U8, name="w1_scale_tile", align_bytes=64)
         picked_scales = held.tile([P, S], U8, name="picked_scales", align_bytes=64)
 
-        nc.vector.memset(table_scales[:], 0)
+        nc.gpsimd.memset(table_scales[:, 0 : T // 8], 0)
+        nc.vector.memset(table_scales[:, T // 8 : T // 4], 0)
         nc.vector.memset(w2_scale_tile[:], 0)
         nc.gpsimd.memset(gelu_warm_in[:], 0.0)
         nc.scalar.activation(gelu_warm_out[:], gelu_warm_in[:], ACT.Gelu_apprx_tanh)
@@ -85,18 +88,18 @@ def tile_list_tabgate_gelu_kernel(tc, tab_words, tab_scales, w1, w2_words, w2_sc
             load_w1(i)
         load_scale_rows(w2_scale_tile, w2_scales[0])
         nc.sync.dma_start(gates[:], gT)
-        bias = held.tile([P, 1], F32, name="bias", tag="warm_then_bias")
         nc.gpsimd.dma_start(bias[:], b.rearrange("(p o) -> p o", o=1))
 
         warm_bank = y_psum.tile([P, WARM_N], F32, name="y_bank")
-        warm_cols = slice(T - WARM_N, T)
+        warm_moving = slice(T - WARM_N, T)
+        warm_stationary = slice(T - SCALE_ALIGN, T - SCALE_ALIGN + WARM_M)
         for repeat in range(WARM_PASSES):
             nc.tensor.matmul_mx(
                 out=warm_bank[0:WARM_M, :],
-                lhsT=table_words[:, T - 64 : T - 64 + WARM_M].bitcast(FP8X4),
-                lhsT_scale=table_scales[:].bitcast(U8)[:, T - 64 : T - 64 + WARM_M],
-                rhs=table_words[:, warm_cols].bitcast(FP8X4),
-                rhs_scale=table_scales[:].bitcast(U8)[:, warm_cols],
+                lhsT=table_words[:, warm_stationary].bitcast(FP8X4),
+                lhsT_scale=table_scales[:].bitcast(U8)[:, warm_stationary],
+                rhs=table_words[:, warm_moving].bitcast(FP8X4),
+                rhs_scale=table_scales[:].bitcast(U8)[:, warm_moving],
                 start=True,
                 stop=True,
             )
@@ -197,9 +200,14 @@ def tile_list_tabgate_gelu_kernel(tc, tab_words, tab_scales, w1, w2_words, w2_sc
             nc.scalar.activation(activated[g][:], y_banks[g][:], ACT.Gelu_apprx_tanh, bias=bias[:])
 
         def gate_and_store(g):
-            s0, s1 = g * GROUP, (g + 1) * GROUP
-            nc.vector.tensor_tensor(result[g][:], gates[:].indirect(list_slice(s0, s1)), activated[g][:], ALU.mult)
-            nc.sync.dma_start(out[:, s0:s1], result[g][:])
+            width = UNIT if g == groups - 1 else GROUP
+            for c0 in range(0, GROUP, width):
+                cols = slice(c0, c0 + width)
+                s0, s1 = g * GROUP + c0, g * GROUP + c0 + width
+                nc.vector.tensor_tensor(
+                    result[g][:, cols], gates[:].indirect(list_slice(s0, s1)), activated[g][:, cols], ALU.mult
+                )
+                nc.sync.dma_start(out[:, s0:s1], result[g][:, cols])
 
         units = S // UNIT
         group_ending_at = {(g + 1) * GROUP_UNITS - 1: g for g in range(groups)}

@@ -27,7 +27,7 @@ UNIT = 128
 GROUP_UNITS = 2
 GROUP = GROUP_UNITS * UNIT
 WORD_GATHERS = [(0, 1024), (1024, 1536)]
-WORDS_AHEAD = 448
+WORDS_AHEAD = 640
 W1_PIECES = [(0, H // 2), (H // 2, H)]
 W1_VECTOR_FROM = 384
 VECTOR_GROUPS = range(1, 4)
@@ -78,17 +78,17 @@ def tile_list_tabgate_gelu_kernel(tc, tab_words, tab_scales, w1, w2_words, w2_sc
             for r in range(4):
                 nc.sync.dma_start(tile[r:P:QUADRANT, :], rows.bitcast(I32)[r:SCALE_ROWS:4, :])
 
-        nc.sync.dma_start(offsets[:], offs)
-        nc.sync.dma_start(w2_codes[:].bitcast(I32), w2_words[0].bitcast(I32))
         words_in_hbm = tab_words[0].rearrange("p n t -> p (n t)").bitcast(I32)
         nc.sync.dma_start(table_words[:, 0:WORDS_AHEAD], words_in_hbm[:, 0:WORDS_AHEAD])
+        nc.sync.dma_start(offsets[:], offs)
+        nc.sync.dma_start(w2_codes[:].bitcast(I32), w2_words[0].bitcast(I32))
         load_scale_rows(table_scales, tab_scales[0])
         nc.sync.dma_start(table_words[:, WORDS_AHEAD:T], words_in_hbm[:, WORDS_AHEAD:T])
         for i in range(len(W1_PIECES)):
             load_w1(i)
         load_scale_rows(w2_scale_tile, w2_scales[0])
+        nc.sync.dma_start(bias[:], b.rearrange("(p o) -> p o", o=1))
         nc.sync.dma_start(gates[:], gT)
-        nc.gpsimd.dma_start(bias[:], b.rearrange("(p o) -> p o", o=1))
 
         warm_bank = y_psum.tile([P, WARM_N], F32, name="y_bank")
         warm_moving = slice(T - WARM_N, T)

@@ -26,7 +26,7 @@ QUADRANT = 32
 UNIT = 128
 GROUP_UNITS = 2
 GROUP = GROUP_UNITS * UNIT
-WORD_GATHERS = [(0, 1024), (1024, 1536)]
+WORD_GATHER = 512
 WORDS_AHEAD = 640
 W1_PIECES = [(0, H // 2), (H // 2, H)]
 W1_VECTOR_FROM = 384
@@ -37,17 +37,18 @@ GATE_LAG = 3
 REUSE_LAG = 3
 H_BANKS = 6
 Y_BANKS = 2
+LAST_BANK_DISTANCE = 3
 WARM_M = 32
 WARM_N = 512
-WARM_PASSES = 5
-SCALE_ALIGN = 64
+EARLY_WARM_PASSES = 4
+LATE_WARM_PASSES = 1
 
 
 def tile_list_tabgate_gelu_kernel(tc, tab_words, tab_scales, w1, w2_words, w2_scales, gT, b, offs, out):
     nc = tc.nc
     with ExitStack() as ctx:
         held = ctx.enter_context(tc.tile_pool(name="held", bufs=1))
-        h_psum = ctx.enter_context(tc.psum_pool(name="h_psum", bufs=H_BANKS))
+        h_psum = ctx.enter_context(tc.psum_pool(name="h_psum", bufs=1))
         y_psum = ctx.enter_context(tc.psum_pool(name="y_psum", bufs=Y_BANKS))
 
         offsets = held.tile([P, S // LIST_ROWS], U16, name="offsets")
@@ -90,20 +91,6 @@ def tile_list_tabgate_gelu_kernel(tc, tab_words, tab_scales, w1, w2_words, w2_sc
         nc.sync.dma_start(bias[:], b.rearrange("(p o) -> p o", o=1))
         nc.sync.dma_start(gates[:], gT)
 
-        warm_bank = y_psum.tile([P, WARM_N], F32, name="y_bank")
-        warm_moving = slice(T - WARM_N, T)
-        warm_stationary = slice(T - SCALE_ALIGN, T - SCALE_ALIGN + WARM_M)
-        for repeat in range(WARM_PASSES):
-            nc.tensor.matmul_mx(
-                out=warm_bank[0:WARM_M, :],
-                lhsT=table_words[:, warm_stationary].bitcast(FP8X4),
-                lhsT_scale=table_scales[:].bitcast(U8)[:, warm_stationary],
-                rhs=table_words[:, warm_moving].bitcast(FP8X4),
-                rhs_scale=table_scales[:].bitcast(U8)[:, warm_moving],
-                start=True,
-                stop=True,
-            )
-
         def regroup_w1(copy, i, c0, c1):
             first = W1_PIECES[i][0]
             copy(
@@ -118,7 +105,7 @@ def tile_list_tabgate_gelu_kernel(tc, tab_words, tab_scales, w1, w2_words, w2_sc
             return offsets[:, s0 // LIST_ROWS : s1 // LIST_ROWS]
 
         def gather_words(c, tag):
-            s0, s1 = WORD_GATHERS[c]
+            s0, s1 = c * WORD_GATHER, (c + 1) * WORD_GATHER
             words = held.tile([P, s1 - s0], U32, name=f"picked_words{c}", tag=tag, align_bytes=64)
             nc.vector.tensor_copy(words[:], table_words[:].bitcast(U32).indirect(list_slice(s0, s1)))
             return words
@@ -135,11 +122,26 @@ def tile_list_tabgate_gelu_kernel(tc, tab_words, tab_scales, w1, w2_words, w2_sc
                     in_=w1_grouped[:, t, m0 : m0 + HALF, :].rearrange("p m j -> p (m j)"),
                 )
 
-        picked_words = [gather_words(0, "picked_words0")]
+        picked_words = [gather_words(0, "picked_words0"), gather_words(1, "picked_words1")]
+
+        def warm_up(passes, warm_bank):
+            for repeat in range(passes):
+                nc.tensor.matmul_mx(
+                    out=warm_bank[0:WARM_M, :],
+                    lhsT=picked_words[0][:, 0:WARM_M].bitcast(FP8X4),
+                    lhsT_scale=picked_scales[:, 0:WARM_M],
+                    rhs=picked_words[0][:, 0:WARM_N].bitcast(FP8X4),
+                    rhs_scale=picked_scales[:, 0:WARM_N],
+                    start=True,
+                    stop=True,
+                )
+
+        warm_up(EARLY_WARM_PASSES, y_psum.tile([P, WARM_N], F32, name="y_bank"))
+
         quantize_w1(0)
         regroup_w1(nc.vector.tensor_copy, len(W1_PIECES) - 1, W1_VECTOR_FROM, H)
         quantize_w1(HALF)
-        picked_words.append(gather_words(1, "w1_then_words"))
+        picked_words.append(gather_words(2, "w1_then_words"))
 
         groups = S // GROUP
         h_scale_tile = [held.tile([P, GROUP], U8, name=f"h_scale_tile{g}", align_bytes=64) for g in range(groups)]
@@ -149,13 +151,16 @@ def tile_list_tabgate_gelu_kernel(tc, tab_words, tab_scales, w1, w2_words, w2_sc
         y_banks = {}
         activated = {}
 
+        def bank_tag(u):
+            return f"h_bank{u % H_BANKS}"
+
         def first_layer(u):
             g, place = divmod(u, GROUP_UNITS)
             if place == 0:
                 h_grouped[g] = held.tile([P, GROUP, PACK], BF16, name=f"h_grouped{g}", align_bytes=64)
-            c = 0 if u * UNIT < WORD_GATHERS[0][1] else 1
-            s0 = u * UNIT - WORD_GATHERS[c][0]
-            bank = h_psum.tile([P, PACK, UNIT], F32, name="h_bank")
+            c, s0 = divmod(u * UNIT, WORD_GATHER)
+            bank_of = u - LAST_BANK_DISTANCE if g == groups - 1 else u
+            bank = h_psum.tile([P, PACK, UNIT], F32, name=f"h_bank{u}", tag=bank_tag(bank_of))
             for t in range(PACK):
                 cols = slice(t * P, (t + 1) * P)
                 nc.tensor.matmul_mx(
@@ -215,6 +220,9 @@ def tile_list_tabgate_gelu_kernel(tc, tab_words, tab_scales, w1, w2_words, w2_sc
         for step in range(units + GATE_LAG):
             if step < units:
                 first_layer(step)
+            if step == units - 1:
+                late_tag = bank_tag(units - GROUP_UNITS - 1)
+                warm_up(LATE_WARM_PASSES, h_psum.tile([P, WARM_N], F32, name="late_bank", tag=late_tag))
             for stage, lag in stages:
                 if step - lag in group_ending_at:
                     stage(group_ending_at[step - lag])

@@ -40,7 +40,7 @@ Y_BANKS = 2
 LAST_BANK_DISTANCE = 3
 WARM_M = 32
 WARM_N = 512
-EARLY_WARM_PASSES = 4
+EARLY_WARM_PASSES = 3
 LATE_WARM_PASSES = 1
 
 

@@ -21,13 +21,13 @@ PACK = 4
 HALF = P // 2
 LIST_ROWS = 16
 SCALE_ROWS = 16
+ROWS_FROM = P - SCALE_ROWS
 QUADRANT = 32
 
 UNIT = 128
 GROUP_UNITS = 2
 GROUP = GROUP_UNITS * UNIT
 WORD_GATHER = 512
-WORDS_AHEAD = 640
 W1_PIECES = [(0, H // 2), (H // 2, H)]
 W1_VECTOR_FROM = 384
 VECTOR_GROUPS = range(1, 4)
@@ -53,8 +53,8 @@ def tile_list_tabgate_gelu_kernel(tc, tab_words, tab_scales, w1, w2_words, w2_sc
 
         offsets = held.tile([P, S // LIST_ROWS], U16, name="offsets")
         table_words = held.tile([P, T], I32, name="table_words", align_bytes=64)
-        table_scales = held.tile([P, T // 4], I32, name="table_scales", align_bytes=64)
-        gates = held.tile([P, T], F32, name="gates", align_bytes=64)
+        scale_window = held.tile([P, T // 4], I32, name="scale_window", tag="scales_then_gates", align_bytes=64)
+        picked_rows = held.tile([P, S], U8, name="picked_rows", align_bytes=64)
         w2_codes = held.tile([P, 2 * M], U8, name="w2_codes", align_bytes=64)
         w2_scale_tile = held.tile([P, M // 4], I32, name="w2_scale_tile", align_bytes=64)
         bias = held.tile([P, 1], F32, name="bias")
@@ -63,12 +63,13 @@ def tile_list_tabgate_gelu_kernel(tc, tab_words, tab_scales, w1, w2_words, w2_sc
         w1_raw = [held.tile([P, PACK, c1 - c0], F32, name=f"w1_raw{c0}", align_bytes=64) for c0, c1 in W1_PIECES]
         w1_grouped = held.tile([P, PACK, P, PACK], BF16, name="w1_grouped", tag="w1_then_words", align_bytes=64)
         w1_scale_tile = held.tile([P, H], U8, name="w1_scale_tile", align_bytes=64)
-        picked_scales = held.tile([P, S], U8, name="picked_scales", align_bytes=64)
+        picked_plane = held.tile([P, S // 4], I32, name="picked_plane", align_bytes=64)
+        picked_scales = picked_plane[:].bitcast(U8)
 
-        nc.gpsimd.memset(table_scales[:, 0 : T // 8], 0)
-        nc.vector.memset(table_scales[:, T // 8 : T // 4], 0)
         nc.vector.memset(w2_scale_tile[:], 0)
+        nc.vector.memset(scale_window[0:ROWS_FROM, :], 0)
         nc.gpsimd.memset(gelu_warm_in[:], 0.0)
+        nc.gpsimd.memset(picked_plane[:], 0)
         nc.scalar.activation(gelu_warm_out[:], gelu_warm_in[:], ACT.Gelu_apprx_tanh)
 
         def load_w1(i):
@@ -80,16 +81,14 @@ def tile_list_tabgate_gelu_kernel(tc, tab_words, tab_scales, w1, w2_words, w2_sc
                 nc.sync.dma_start(tile[r:P:QUADRANT, :], rows.bitcast(I32)[r:SCALE_ROWS:4, :])
 
         words_in_hbm = tab_words[0].rearrange("p n t -> p (n t)").bitcast(I32)
-        nc.sync.dma_start(table_words[:, 0:WORDS_AHEAD], words_in_hbm[:, 0:WORDS_AHEAD])
+        nc.sync.dma_start(scale_window[ROWS_FROM:P, :], tab_scales[0].bitcast(I32))
         nc.sync.dma_start(offsets[:], offs)
+        nc.sync.dma_start(table_words[:], words_in_hbm)
+        load_scale_rows(w2_scale_tile, w2_scales[0])
         nc.sync.dma_start(w2_codes[:].bitcast(I32), w2_words[0].bitcast(I32))
-        load_scale_rows(table_scales, tab_scales[0])
-        nc.sync.dma_start(table_words[:, WORDS_AHEAD:T], words_in_hbm[:, WORDS_AHEAD:T])
         for i in range(len(W1_PIECES)):
             load_w1(i)
-        load_scale_rows(w2_scale_tile, w2_scales[0])
         nc.sync.dma_start(bias[:], b.rearrange("(p o) -> p o", o=1))
-        nc.sync.dma_start(gates[:], gT)
 
         def regroup_w1(copy, i, c0, c1):
             first = W1_PIECES[i][0]
@@ -110,7 +109,11 @@ def tile_list_tabgate_gelu_kernel(tc, tab_words, tab_scales, w1, w2_words, w2_sc
             nc.vector.tensor_copy(words[:], table_words[:].bitcast(U32).indirect(list_slice(s0, s1)))
             return words
 
-        nc.vector.tensor_copy(picked_scales[:], table_scales[:].bitcast(U8).indirect(offsets[:]))
+        nc.vector.tensor_copy(picked_rows[:], scale_window[:].bitcast(U8).indirect(offsets[:]))
+        for r in range(4):
+            nc.sync.dma_start(picked_plane[r:P:QUADRANT, :], picked_rows[:].bitcast(I32)[ROWS_FROM + r : P : 4, :])
+        gates = held.tile([P, T], F32, name="gates", tag="scales_then_gates", align_bytes=64)
+        nc.sync.dma_start(gates[:], gT)
         w1_codes = held.tile([P, H], U32, name="w1_codes", align_bytes=64)
 
         def quantize_w1(m0):
@@ -129,9 +132,9 @@ def tile_list_tabgate_gelu_kernel(tc, tab_words, tab_scales, w1, w2_words, w2_sc
                 nc.tensor.matmul_mx(
                     out=warm_bank[0:WARM_M, :],
                     lhsT=picked_words[0][:, 0:WARM_M].bitcast(FP8X4),
-                    lhsT_scale=picked_scales[:, 0:WARM_M],
+                    lhsT_scale=picked_rows[:, 0:WARM_M],
                     rhs=picked_words[0][:, 0:WARM_N].bitcast(FP8X4),
-                    rhs_scale=picked_scales[:, 0:WARM_N],
+                    rhs_scale=picked_rows[:, 0:WARM_N],
                     start=True,
                     stop=True,
                 )

@@ -21,7 +21,10 @@ PACK = 4
 HALF = P // 2
 LIST_ROWS = 16
 SCALE_ROWS = 16
-ROWS_FROM = P - SCALE_ROWS
+ROWS_FROM = 32
+ROWS_STEP = 4
+ROWS_END = ROWS_FROM + ROWS_STEP * SCALE_ROWS
+WORDS_AHEAD = 640
 QUADRANT = 32
 
 UNIT = 128
@@ -67,7 +70,8 @@ def tile_list_tabgate_gelu_kernel(tc, tab_words, tab_scales, w1, w2_words, w2_sc
         picked_scales = picked_plane[:].bitcast(U8)
 
         nc.vector.memset(w2_scale_tile[:], 0)
-        nc.vector.memset(scale_window[0:ROWS_FROM, :], 0)
+        nc.gpsimd.memset(scale_window[:, 0 : T // 8], 0)
+        nc.vector.memset(scale_window[:, T // 8 : T // 4], 0)
         nc.gpsimd.memset(gelu_warm_in[:], 0.0)
         nc.gpsimd.memset(picked_plane[:], 0)
         nc.scalar.activation(gelu_warm_out[:], gelu_warm_in[:], ACT.Gelu_apprx_tanh)
@@ -81,13 +85,14 @@ def tile_list_tabgate_gelu_kernel(tc, tab_words, tab_scales, w1, w2_words, w2_sc
                 nc.sync.dma_start(tile[r:P:QUADRANT, :], rows.bitcast(I32)[r:SCALE_ROWS:4, :])
 
         words_in_hbm = tab_words[0].rearrange("p n t -> p (n t)").bitcast(I32)
-        nc.sync.dma_start(scale_window[ROWS_FROM:P, :], tab_scales[0].bitcast(I32))
+        nc.sync.dma_start(table_words[:, 0:WORDS_AHEAD], words_in_hbm[:, 0:WORDS_AHEAD])
         nc.sync.dma_start(offsets[:], offs)
-        nc.sync.dma_start(table_words[:], words_in_hbm)
         load_scale_rows(w2_scale_tile, w2_scales[0])
-        nc.sync.dma_start(w2_codes[:].bitcast(I32), w2_words[0].bitcast(I32))
+        nc.sync.dma_start(scale_window[ROWS_FROM:ROWS_END:ROWS_STEP, :], tab_scales[0].bitcast(I32))
+        nc.sync.dma_start(table_words[:, WORDS_AHEAD:T], words_in_hbm[:, WORDS_AHEAD:T])
         for i in range(len(W1_PIECES)):
             load_w1(i)
+        nc.sync.dma_start(w2_codes[:].bitcast(I32), w2_words[0].bitcast(I32))
         nc.sync.dma_start(bias[:], b.rearrange("(p o) -> p o", o=1))
 
         def regroup_w1(copy, i, c0, c1):
@@ -111,7 +116,7 @@ def tile_list_tabgate_gelu_kernel(tc, tab_words, tab_scales, w1, w2_words, w2_sc
 
         nc.vector.tensor_copy(picked_rows[:], scale_window[:].bitcast(U8).indirect(offsets[:]))
         for r in range(4):
-            nc.sync.dma_start(picked_plane[r:P:QUADRANT, :], picked_rows[:].bitcast(I32)[ROWS_FROM + r : P : 4, :])
+            nc.sync.dma_start(picked_plane[r:P:QUADRANT, :], picked_rows[:].bitcast(I32)[ROWS_FROM + ROWS_STEP * r : ROWS_END : 4 * ROWS_STEP, :])
         gates = held.tile([P, T], F32, name="gates", tag="scales_then_gates", align_bytes=64)
         nc.sync.dma_start(gates[:], gT)
         w1_codes = held.tile([P, H], U32, name="w1_codes", align_bytes=64)

@@ -69,11 +69,10 @@ def tile_list_tabgate_gelu_kernel(tc, tab_words, tab_scales, w1, w2_words, w2_sc
         picked_plane = held.tile([P, S // 4], I32, name="picked_plane", align_bytes=64)
         picked_scales = picked_plane[:].bitcast(U8)
 
+        nc.vector.memset(scale_window[:].bitcast(F32), 0.0)
         nc.vector.memset(w2_scale_tile[:], 0)
-        nc.gpsimd.memset(scale_window[:, 0 : T // 8], 0)
-        nc.vector.memset(scale_window[:, T // 8 : T // 4], 0)
-        nc.gpsimd.memset(gelu_warm_in[:], 0.0)
-        nc.gpsimd.memset(picked_plane[:], 0)
+        nc.vector.memset(gelu_warm_in[:], 0.0)
+        nc.vector.memset(picked_plane[:], 0)
         nc.scalar.activation(gelu_warm_out[:], gelu_warm_in[:], ACT.Gelu_apprx_tanh)
 
         def load_w1(i):
@@ -87,12 +86,12 @@ def tile_list_tabgate_gelu_kernel(tc, tab_words, tab_scales, w1, w2_words, w2_sc
         words_in_hbm = tab_words[0].rearrange("p n t -> p (n t)").bitcast(I32)
         nc.sync.dma_start(table_words[:, 0:WORDS_AHEAD], words_in_hbm[:, 0:WORDS_AHEAD])
         nc.sync.dma_start(offsets[:], offs)
-        load_scale_rows(w2_scale_tile, w2_scales[0])
+        nc.sync.dma_start(w2_codes[:].bitcast(I32), w2_words[0].bitcast(I32))
         nc.sync.dma_start(scale_window[ROWS_FROM:ROWS_END:ROWS_STEP, :], tab_scales[0].bitcast(I32))
         nc.sync.dma_start(table_words[:, WORDS_AHEAD:T], words_in_hbm[:, WORDS_AHEAD:T])
+        load_scale_rows(w2_scale_tile, w2_scales[0])
         for i in range(len(W1_PIECES)):
             load_w1(i)
-        nc.sync.dma_start(w2_codes[:].bitcast(I32), w2_words[0].bitcast(I32))
         nc.sync.dma_start(bias[:], b.rearrange("(p o) -> p o", o=1))
 
         def regroup_w1(copy, i, c0, c1):

@@ -24,7 +24,7 @@ SCALE_ROWS = 16
 ROWS_FROM = 32
 ROWS_STEP = 4
 ROWS_END = ROWS_FROM + ROWS_STEP * SCALE_ROWS
-WORDS_AHEAD = 640
+WORDS_AHEAD = 832
 QUADRANT = 32
 
 UNIT = 128
@@ -43,6 +43,7 @@ Y_BANKS = 2
 LAST_BANK_DISTANCE = 3
 WARM_M = 32
 WARM_N = 512
+FIRST_WARM_PASSES = 1
 EARLY_WARM_PASSES = 3
 LATE_WARM_PASSES = 1
 
@@ -131,19 +132,21 @@ def tile_list_tabgate_gelu_kernel(tc, tab_words, tab_scales, w1, w2_words, w2_sc
 
         picked_words = [gather_words(0, "picked_words0"), gather_words(1, "picked_words1")]
 
-        def warm_up(passes, warm_bank):
+        def warm_up(passes, warm_bank, words):
             for repeat in range(passes):
                 nc.tensor.matmul_mx(
                     out=warm_bank[0:WARM_M, :],
-                    lhsT=picked_words[0][:, 0:WARM_M].bitcast(FP8X4),
+                    lhsT=words[:, 0:WARM_M].bitcast(FP8X4),
                     lhsT_scale=picked_rows[:, 0:WARM_M],
-                    rhs=picked_words[0][:, 0:WARM_N].bitcast(FP8X4),
+                    rhs=words[:, 0:WARM_N].bitcast(FP8X4),
                     rhs_scale=picked_rows[:, 0:WARM_N],
                     start=True,
                     stop=True,
                 )
 
-        warm_up(EARLY_WARM_PASSES, y_psum.tile([P, WARM_N], F32, name="y_bank"))
+        early_bank = y_psum.tile([P, WARM_N], F32, name="y_bank")
+        warm_up(FIRST_WARM_PASSES, early_bank, table_words[:, T - WARM_N : T])
+        warm_up(EARLY_WARM_PASSES, early_bank, picked_words[0])
 
         quantize_w1(0)
         regroup_w1(nc.vector.tensor_copy, len(W1_PIECES) - 1, W1_VECTOR_FROM, H)
@@ -229,7 +232,7 @@ def tile_list_tabgate_gelu_kernel(tc, tab_words, tab_scales, w1, w2_words, w2_sc
                 first_layer(step)
             if step == units - 1:
                 late_tag = bank_tag(units - GROUP_UNITS - 1)
-                warm_up(LATE_WARM_PASSES, h_psum.tile([P, WARM_N], F32, name="late_bank", tag=late_tag))
+                warm_up(LATE_WARM_PASSES, h_psum.tile([P, WARM_N], F32, name="late_bank", tag=late_tag), picked_words[0])
             for stage, lag in stages:
                 if step - lag in group_ending_at:
                     stage(group_ending_at[step - lag])

@@ -32,7 +32,7 @@ GROUP_UNITS = 2
 GROUP = GROUP_UNITS * UNIT
 WORD_GATHER = 512
 W1_PIECES = [(0, H // 2), (H // 2, H)]
-W1_VECTOR_FROM = 384
+W1_VECTOR_FROM = 320
 VECTOR_GROUPS = range(1, 4)
 SECOND_LAG = 1
 GELU_LAG = 2
@@ -64,13 +64,13 @@ def tile_list_tabgate_gelu_kernel(tc, tab_words, tab_scales, w1, w2_words, w2_sc
         bias = held.tile([P, 1], F32, name="bias")
         gelu_warm_in = held.tile([P, 1], F32, name="gelu_warm_in")
         gelu_warm_out = held.tile([P, 1], F32, name="gelu_warm_out")
-        w1_raw = [held.tile([P, PACK, c1 - c0], F32, name=f"w1_raw{c0}", align_bytes=64) for c0, c1 in W1_PIECES]
-        w1_grouped = held.tile([P, PACK, P, PACK], BF16, name="w1_grouped", tag="w1_then_words", align_bytes=64)
+        w1_raw = [held.tile([P, PACK, c1 - c0], F32, name=f"w1_raw{c0}", tag=f"w1_raw{c0}", align_bytes=64) for c0, c1 in W1_PIECES]
+        w1_grouped = held.tile([P, PACK, P, PACK], BF16, name="w1_grouped", align_bytes=64)
         w1_scale_tile = held.tile([P, H], U8, name="w1_scale_tile", align_bytes=64)
         picked_plane = held.tile([P, S // 4], I32, name="picked_plane", align_bytes=64)
         picked_scales = picked_plane[:].bitcast(U8)
 
-        nc.vector.memset(scale_window[:].bitcast(F32), 0.0)
+        nc.vector.memset(scale_window[:], 0)
         nc.vector.memset(w2_scale_tile[:], 0)
         nc.vector.memset(gelu_warm_in[:], 0.0)
         nc.vector.memset(picked_plane[:], 0)
@@ -151,7 +151,7 @@ def tile_list_tabgate_gelu_kernel(tc, tab_words, tab_scales, w1, w2_words, w2_sc
         quantize_w1(0)
         regroup_w1(nc.vector.tensor_copy, len(W1_PIECES) - 1, W1_VECTOR_FROM, H)
         quantize_w1(HALF)
-        picked_words.append(gather_words(2, "w1_then_words"))
+        picked_words.append(gather_words(2, f"w1_raw{W1_PIECES[-1][0]}"))
 
         groups = S // GROUP
         h_scale_tile = [held.tile([P, GROUP], U8, name=f"h_scale_tile{g}", align_bytes=64) for g in range(groups)]

@@ -56,18 +56,18 @@ def tile_list_tabgate_gelu_kernel(tc, tab_words, tab_scales, w1, w2_words, w2_sc
         y_psum = ctx.enter_context(tc.psum_pool(name="y_psum", bufs=Y_BANKS))
 
         offsets = held.tile([P, S // LIST_ROWS], U16, name="offsets")
-        table_words = held.tile([P, T], I32, name="table_words", align_bytes=64)
-        scale_window = held.tile([P, T // 4], I32, name="scale_window", tag="scales_then_gates", align_bytes=64)
-        picked_rows = held.tile([P, S], U8, name="picked_rows", align_bytes=64)
-        w2_codes = held.tile([P, 2 * M], U8, name="w2_codes", align_bytes=64)
-        w2_scale_tile = held.tile([P, M // 4], I32, name="w2_scale_tile", align_bytes=64)
+        table_words = held.tile([P, T], I32, name="table_words", align_bytes=256)
+        scale_window = held.tile([P, T // 4], I32, name="scale_window", tag="scales_then_gates", align_bytes=256)
+        picked_rows = held.tile([P, S], U8, name="picked_rows", align_bytes=256)
+        w2_codes = held.tile([P, 2 * M], U8, name="w2_codes", align_bytes=256)
+        w2_scale_tile = held.tile([P, M // 4], I32, name="w2_scale_tile", align_bytes=256)
         bias = held.tile([P, 1], F32, name="bias")
         gelu_warm_in = held.tile([P, 1], F32, name="gelu_warm_in")
         gelu_warm_out = held.tile([P, 1], F32, name="gelu_warm_out")
-        w1_raw = [held.tile([P, PACK, c1 - c0], F32, name=f"w1_raw{c0}", tag=f"w1_raw{c0}", align_bytes=64) for c0, c1 in W1_PIECES]
-        w1_grouped = held.tile([P, PACK, P, PACK], BF16, name="w1_grouped", align_bytes=64)
-        w1_scale_tile = held.tile([P, H], U8, name="w1_scale_tile", align_bytes=64)
-        picked_plane = held.tile([P, S // 4], I32, name="picked_plane", align_bytes=64)
+        w1_raw = [held.tile([P, PACK, c1 - c0], F32, name=f"w1_raw{c0}", tag=f"w1_raw{c0}", align_bytes=256) for c0, c1 in W1_PIECES]
+        w1_grouped = held.tile([P, PACK, P, PACK], BF16, name="w1_grouped", align_bytes=256)
+        w1_scale_tile = held.tile([P, H], U8, name="w1_scale_tile", align_bytes=256)
+        picked_plane = held.tile([P, S // 4], I32, name="picked_plane", align_bytes=256)
         picked_scales = picked_plane[:].bitcast(U8)
 
         nc.vector.memset(scale_window[:], 0)
@@ -110,16 +110,16 @@ def tile_list_tabgate_gelu_kernel(tc, tab_words, tab_scales, w1, w2_words, w2_sc
 
         def gather_words(c, tag):
             s0, s1 = c * WORD_GATHER, (c + 1) * WORD_GATHER
-            words = held.tile([P, s1 - s0], U32, name=f"picked_words{c}", tag=tag, align_bytes=64)
+            words = held.tile([P, s1 - s0], U32, name=f"picked_words{c}", tag=tag, align_bytes=256)
             nc.vector.tensor_copy(words[:], table_words[:].bitcast(U32).indirect(list_slice(s0, s1)))
             return words
 
         nc.vector.tensor_copy(picked_rows[:], scale_window[:].bitcast(U8).indirect(offsets[:]))
         for r in range(4):
             nc.sync.dma_start(picked_plane[r:P:QUADRANT, :], picked_rows[:].bitcast(I32)[ROWS_FROM + ROWS_STEP * r : ROWS_END : 4 * ROWS_STEP, :])
-        gates = held.tile([P, T], F32, name="gates", tag="scales_then_gates", align_bytes=64)
+        gates = held.tile([P, T], F32, name="gates", tag="scales_then_gates", align_bytes=256)
         nc.sync.dma_start(gates[:], gT)
-        w1_codes = held.tile([P, H], U32, name="w1_codes", align_bytes=64)
+        w1_codes = held.tile([P, H], U32, name="w1_codes", align_bytes=256)
 
         def quantize_w1(m0):
             for t in range(PACK):
@@ -154,8 +154,8 @@ def tile_list_tabgate_gelu_kernel(tc, tab_words, tab_scales, w1, w2_words, w2_sc
         picked_words.append(gather_words(2, f"w1_raw{W1_PIECES[-1][0]}"))
 
         groups = S // GROUP
-        h_scale_tile = [held.tile([P, GROUP], U8, name=f"h_scale_tile{g}", align_bytes=64) for g in range(groups)]
-        result = [held.tile([P, GROUP], F32, name=f"result{g}", align_bytes=64) for g in range(groups)]
+        h_scale_tile = [held.tile([P, GROUP], U8, name=f"h_scale_tile{g}", align_bytes=256) for g in range(groups)]
+        result = [held.tile([P, GROUP], F32, name=f"result{g}", align_bytes=256) for g in range(groups)]
         h_grouped = {}
         h_codes = {}
         y_banks = {}
@@ -167,7 +167,7 @@ def tile_list_tabgate_gelu_kernel(tc, tab_words, tab_scales, w1, w2_words, w2_sc
         def first_layer(u):
             g, place = divmod(u, GROUP_UNITS)
             if place == 0:
-                h_grouped[g] = held.tile([P, GROUP, PACK], BF16, name=f"h_grouped{g}", align_bytes=64)
+                h_grouped[g] = held.tile([P, GROUP, PACK], BF16, name=f"h_grouped{g}", align_bytes=256)
             c, s0 = divmod(u * UNIT, WORD_GATHER)
             bank_of = u - LAST_BANK_DISTANCE if g == groups - 1 else u
             bank = h_psum.tile([P, PACK, UNIT], F32, name=f"h_bank{u}", tag=bank_tag(bank_of))
@@ -191,7 +191,7 @@ def tile_list_tabgate_gelu_kernel(tc, tab_words, tab_scales, w1, w2_words, w2_sc
 
         def quantize_h(g):
             tag = f"activated{g - REUSE_LAG}" if g >= REUSE_LAG else f"h_codes{g}"
-            h_codes[g] = held.tile([P, GROUP], U32, name=f"h_codes{g}", tag=tag, align_bytes=64)
+            h_codes[g] = held.tile([P, GROUP], U32, name=f"h_codes{g}", tag=tag, align_bytes=256)
             nc.vector.quantize_mx(
                 out=h_codes[g][:].bitcast(FP8X4),
                 scales=h_scale_tile[g][:],
@@ -211,7 +211,7 @@ def tile_list_tabgate_gelu_kernel(tc, tab_words, tab_scales, w1, w2_words, w2_sc
             )
 
         def gelu(g):
-            activated[g] = held.tile([P, GROUP], F32, name=f"activated{g}", tag=f"activated{g}", align_bytes=64)
+            activated[g] = held.tile([P, GROUP], F32, name=f"activated{g}", tag=f"activated{g}", align_bytes=256)
             nc.scalar.activation(activated[g][:], y_banks[g][:], ACT.Gelu_apprx_tanh, bias=bias[:])
 
         def gate_and_store(g):

@@ -198,27 +198,35 @@ def tile_list_tabgate_gelu_kernel(tc, tab_words, tab_scales, w1, w2_words, w2_sc
                 in_=h_grouped[g][:].rearrange("p n t -> p (n t)"),
             )
 
+        def pieces(g):
+            width = UNIT if g == groups - 1 else GROUP
+            return [slice(c0, c0 + width) for c0 in range(0, GROUP, width)]
+
         def second_layer(g):
-            y_banks[g] = y_psum.tile([P, GROUP], F32, name="y_bank")
-            nc.tensor.matmul_mx(
-                out=y_banks[g][:],
-                lhsT=w2_codes[:].bitcast(FP4X4),
-                lhsT_scale=w2_scale_tile[:].bitcast(U8),
-                rhs=h_codes[g][:].bitcast(FP8X4),
-                rhs_scale=h_scale_tile[g][:],
-                start=True,
-                stop=True,
-            )
+            for cols in pieces(g):
+                if g == groups - 1:
+                    free_tag = bank_tag((g * GROUP + cols.start) // UNIT)
+                    y_banks[g, cols.start] = h_psum.tile([P, GROUP], F32, name=f"last_y_bank{cols.start}", tag=free_tag)
+                else:
+                    y_banks[g, cols.start] = y_psum.tile([P, GROUP], F32, name="y_bank")
+                nc.tensor.matmul_mx(
+                    out=y_banks[g, cols.start][:, cols],
+                    lhsT=w2_codes[:].bitcast(FP4X4),
+                    lhsT_scale=w2_scale_tile[:].bitcast(U8),
+                    rhs=h_codes[g][:, cols].bitcast(FP8X4),
+                    rhs_scale=h_scale_tile[g][:, cols],
+                    start=True,
+                    stop=True,
+                )
 
         def gelu(g):
             activated[g] = held.tile([P, GROUP], F32, name=f"activated{g}", tag=f"activated{g}", align_bytes=256)
-            nc.scalar.activation(activated[g][:], y_banks[g][:], ACT.Gelu_apprx_tanh, bias=bias[:])
+            for cols in pieces(g):
+                nc.scalar.activation(activated[g][:, cols], y_banks[g, cols.start][:, cols], ACT.Gelu_apprx_tanh, bias=bias[:])
 
         def gate_and_store(g):
-            width = UNIT if g == groups - 1 else GROUP
-            for c0 in range(0, GROUP, width):
-                cols = slice(c0, c0 + width)
-                s0, s1 = g * GROUP + c0, g * GROUP + c0 + width
+            for cols in pieces(g):
+                s0, s1 = g * GROUP + cols.start, g * GROUP + cols.stop
                 nc.vector.tensor_tensor(
                     result[g][:, cols], gates[:].indirect(list_slice(s0, s1)), activated[g][:, cols], ALU.mult
                 )

@@ -167,7 +167,7 @@ def tile_list_tabgate_gelu_kernel(tc, tab_words, tab_scales, w1, w2_words, w2_sc
         def first_layer(u):
             g, place = divmod(u, GROUP_UNITS)
             if place == 0:
-                h_grouped[g] = held.tile([P, GROUP, PACK], BF16, name=f"h_grouped{g}", align_bytes=256)
+                h_grouped[g] = held.tile([P, GROUP, PACK], BF16, name=f"h_grouped{g}", tag=f"h_grouped{g}", align_bytes=256)
             c, s0 = divmod(u * UNIT, WORD_GATHER)
             bank_of = u - LAST_BANK_DISTANCE if g == groups - 1 else u
             bank = h_psum.tile([P, PACK, UNIT], F32, name=f"h_bank{u}", tag=bank_tag(bank_of))
@@ -190,7 +190,12 @@ def tile_list_tabgate_gelu_kernel(tc, tab_words, tab_scales, w1, w2_words, w2_sc
                 nc.scalar.activation(interleaved, sums, ACT.Relu)
 
         def quantize_h(g):
-            tag = f"activated{g - REUSE_LAG}" if g >= REUSE_LAG else f"h_codes{g}"
+            if g == groups - 1:
+                tag = f"h_grouped{g - 1}"
+            elif g >= REUSE_LAG:
+                tag = f"activated{g - REUSE_LAG}"
+            else:
+                tag = f"h_codes{g}"
             h_codes[g] = held.tile([P, GROUP], U32, name=f"h_codes{g}", tag=tag, align_bytes=256)
             nc.vector.quantize_mx(
                 out=h_codes[g][:].bitcast(FP8X4),
@@ -234,13 +239,23 @@ def tile_list_tabgate_gelu_kernel(tc, tab_words, tab_scales, w1, w2_words, w2_sc
 
         units = S // UNIT
         group_ending_at = {(g + 1) * GROUP_UNITS - 1: g for g in range(groups)}
-        stages = ((gate_and_store, GATE_LAG), (quantize_h, 0), (second_layer, SECOND_LAG), (gelu, GELU_LAG))
-        for step in range(units + GATE_LAG):
-            if step < units:
-                first_layer(step)
+
+        def finish(first, end):
+            for g in range(first, end):
+                gelu(g)
+                gate_and_store(g)
+
+        for step in range(units):
+            first_layer(step)
             if step == units - 1:
                 late_tag = bank_tag(units - GROUP_UNITS - 1)
                 warm_up(LATE_WARM_PASSES, h_psum.tile([P, WARM_N], F32, name="late_bank", tag=late_tag), picked_words[0])
-            for stage, lag in stages:
-                if step - lag in group_ending_at:
-                    stage(group_ending_at[step - lag])
+            if step in group_ending_at:
+                g = group_ending_at[step]
+                if g == REUSE_LAG:
+                    finish(0, REUSE_LAG - 1)
+                quantize_h(g)
+                second_layer(g)
+                if g == groups - 2:
+                    finish(REUSE_LAG - 1, REUSE_LAG)
+        finish(REUSE_LAG, groups)

from contextlib import ExitStack

import concourse.mybir as mybir

K, M, T, S, H = 512, 128, 4096, 1536, 512
FLOPS = 2 * K * H * S + 2 * H * M * S

F32 = mybir.dt.float32
BF16 = mybir.dt.bfloat16
I32 = mybir.dt.int32
U32 = mybir.dt.uint32
U16 = mybir.dt.uint16
U8 = mybir.dt.uint8
FP8X4 = mybir.dt.float8_e4m3fn_x4
FP4X4 = mybir.dt.float4_e2m1fn_x4
ACT = mybir.ActivationFunctionType
ALU = mybir.AluOpType

P = 128
PACK = 4
HALF = P // 2
LIST_ROWS = 16
SCALE_ROWS = 16
ROWS_FROM = 32
ROWS_STEP = 4
ROWS_END = ROWS_FROM + ROWS_STEP * SCALE_ROWS
WORDS_AHEAD = 832
QUADRANT = 32

UNIT = 128
GROUP_UNITS = 2
GROUP = GROUP_UNITS * UNIT
WORD_GATHER = 512
W1_PIECES = [(0, H // 2), (H // 2, H)]
W1_VECTOR_FROM = 320
VECTOR_GROUPS = range(1, 4)
SECOND_LAG = 1
GELU_LAG = 2
GATE_LAG = 3
REUSE_LAG = 3
H_BANKS = 6
Y_BANKS = 2
LAST_BANK_DISTANCE = 3
WARM_M = 32
WARM_N = 512
FIRST_WARM_PASSES = 1
EARLY_WARM_PASSES = 3
LATE_WARM_PASSES = 1


def tile_list_tabgate_gelu_kernel(tc, tab_words, tab_scales, w1, w2_words, w2_scales, gT, b, offs, out):
    nc = tc.nc
    with ExitStack() as ctx:
        held = ctx.enter_context(tc.tile_pool(name="held", bufs=1))
        h_psum = ctx.enter_context(tc.psum_pool(name="h_psum", bufs=1))
        y_psum = ctx.enter_context(tc.psum_pool(name="y_psum", bufs=Y_BANKS))

        offsets = held.tile([P, S // LIST_ROWS], U16, name="offsets")
        table_words = held.tile([P, T], I32, name="table_words", align_bytes=256)
        scale_window = held.tile([P, T // 4], I32, name="scale_window", tag="scales_then_gates", align_bytes=256)
        picked_rows = held.tile([P, S], U8, name="picked_rows", align_bytes=256)
        w2_codes = held.tile([P, 2 * M], U8, name="w2_codes", align_bytes=256)
        w2_scale_tile = held.tile([P, M // 4], I32, name="w2_scale_tile", align_bytes=256)
        bias = held.tile([P, 1], F32, name="bias")
        gelu_warm_in = held.tile([P, 1], F32, name="gelu_warm_in")
        gelu_warm_out = held.tile([P, 1], F32, name="gelu_warm_out")
        w1_raw = [held.tile([P, PACK, c1 - c0], F32, name=f"w1_raw{c0}", tag=f"w1_raw{c0}", align_bytes=256) for c0, c1 in W1_PIECES]
        w1_grouped = held.tile([P, PACK, P, PACK], BF16, name="w1_grouped", align_bytes=256)
        w1_scale_tile = held.tile([P, H], U8, name="w1_scale_tile", align_bytes=256)
        picked_plane = held.tile([P, S // 4], I32, name="picked_plane", align_bytes=256)
        picked_scales = picked_plane[:].bitcast(U8)

        nc.vector.memset(scale_window[:], 0)
        nc.vector.memset(w2_scale_tile[:], 0)
        nc.vector.memset(gelu_warm_in[:], 0.0)
        nc.vector.memset(picked_plane[:], 0)
        nc.scalar.activation(gelu_warm_out[:], gelu_warm_in[:], ACT.Gelu_apprx_tanh)

        def load_w1(i):
            c0, c1 = W1_PIECES[i]
            nc.sync.dma_start(w1_raw[i][:], w1.rearrange("(p j) c -> p j c", j=PACK)[:, :, c0:c1])

        def load_scale_rows(tile, rows):
            for r in range(4):
                nc.sync.dma_start(tile[r:P:QUADRANT, :], rows.bitcast(I32)[r:SCALE_ROWS:4, :])

        words_in_hbm = tab_words[0].rearrange("p n t -> p (n t)").bitcast(I32)
        nc.sync.dma_start(table_words[:, 0:WORDS_AHEAD], words_in_hbm[:, 0:WORDS_AHEAD])
        nc.sync.dma_start(offsets[:], offs)
        nc.sync.dma_start(w2_codes[:].bitcast(I32), w2_words[0].bitcast(I32))
        nc.sync.dma_start(scale_window[ROWS_FROM:ROWS_END:ROWS_STEP, :], tab_scales[0].bitcast(I32))
        nc.sync.dma_start(table_words[:, WORDS_AHEAD:T], words_in_hbm[:, WORDS_AHEAD:T])
        load_scale_rows(w2_scale_tile, w2_scales[0])
        for i in range(len(W1_PIECES)):
            load_w1(i)
        nc.sync.dma_start(bias[:], b.rearrange("(p o) -> p o", o=1))

        def regroup_w1(copy, i, c0, c1):
            first = W1_PIECES[i][0]
            copy(
                w1_grouped[:, :, c0 // PACK : c1 // PACK, :].rearrange("p t m j -> p m j t"),
                w1_raw[i][:, :, c0 - first : c1 - first].rearrange("p j (m t) -> p m j t", t=PACK),
            )

        for i, (c0, c1) in enumerate(W1_PIECES):
            regroup_w1(nc.scalar.copy, i, c0, min(c1, W1_VECTOR_FROM))

        def list_slice(s0, s1):
            return offsets[:, s0 // LIST_ROWS : s1 // LIST_ROWS]

        def gather_words(c, tag):
            s0, s1 = c * WORD_GATHER, (c + 1) * WORD_GATHER
            words = held.tile([P, s1 - s0], U32, name=f"picked_words{c}", tag=tag, align_bytes=256)
            nc.vector.tensor_copy(words[:], table_words[:].bitcast(U32).indirect(list_slice(s0, s1)))
            return words

        nc.vector.tensor_copy(picked_rows[:], scale_window[:].bitcast(U8).indirect(offsets[:]))
        for r in range(4):
            nc.sync.dma_start(picked_plane[r:P:QUADRANT, :], picked_rows[:].bitcast(I32)[ROWS_FROM + ROWS_STEP * r : ROWS_END : 4 * ROWS_STEP, :])
        gates = held.tile([P, T], F32, name="gates", tag="scales_then_gates", align_bytes=256)
        nc.sync.dma_start(gates[:], gT)
        w1_codes = held.tile([P, H], U32, name="w1_codes", align_bytes=256)

        def quantize_w1(m0):
            for t in range(PACK):
                cols = slice(t * P + m0, t * P + m0 + HALF)
                nc.vector.quantize_mx(
                    out=w1_codes[:, cols].bitcast(FP8X4),
                    scales=w1_scale_tile[:, cols],
                    in_=w1_grouped[:, t, m0 : m0 + HALF, :].rearrange("p m j -> p (m j)"),
                )

        picked_words = [gather_words(0, "picked_words0"), gather_words(1, "picked_words1")]

        def warm_up(passes, warm_bank, words):
            for repeat in range(passes):
                nc.tensor.matmul_mx(
                    out=warm_bank[0:WARM_M, :],
                    lhsT=words[:, 0:WARM_M].bitcast(FP8X4),
                    lhsT_scale=picked_rows[:, 0:WARM_M],
                    rhs=words[:, 0:WARM_N].bitcast(FP8X4),
                    rhs_scale=picked_rows[:, 0:WARM_N],
                    start=True,
                    stop=True,
                )

        early_bank = y_psum.tile([P, WARM_N], F32, name="y_bank")
        warm_up(FIRST_WARM_PASSES, early_bank, table_words[:, T - WARM_N : T])
        warm_up(EARLY_WARM_PASSES, early_bank, picked_words[0])

        quantize_w1(0)
        regroup_w1(nc.vector.tensor_copy, len(W1_PIECES) - 1, W1_VECTOR_FROM, H)
        quantize_w1(HALF)
        picked_words.append(gather_words(2, f"w1_raw{W1_PIECES[-1][0]}"))

        groups = S // GROUP
        h_scale_tile = [held.tile([P, GROUP], U8, name=f"h_scale_tile{g}", align_bytes=256) for g in range(groups)]
        result = [held.tile([P, GROUP], F32, name=f"result{g}", align_bytes=256) for g in range(groups)]
        h_grouped = {}
        h_codes = {}
        y_banks = {}
        activated = {}

        def bank_tag(u):
            return f"h_bank{u % H_BANKS}"

        def first_layer(u):
            g, place = divmod(u, GROUP_UNITS)
            if place == 0:
                h_grouped[g] = held.tile([P, GROUP, PACK], BF16, name=f"h_grouped{g}", tag=f"h_grouped{g}", align_bytes=256)
            c, s0 = divmod(u * UNIT, WORD_GATHER)
            bank_of = u - LAST_BANK_DISTANCE if g == groups - 1 else u
            bank = h_psum.tile([P, PACK, UNIT], F32, name=f"h_bank{u}", tag=bank_tag(bank_of))
            for t in range(PACK):
                cols = slice(t * P, (t + 1) * P)
                nc.tensor.matmul_mx(
                    out=bank[:, t, :],
                    lhsT=w1_codes[:, cols].bitcast(FP8X4),
                    lhsT_scale=w1_scale_tile[:, cols],
                    rhs=picked_words[c][:, s0 : s0 + UNIT].bitcast(FP8X4),
                    rhs_scale=picked_scales[:, u * UNIT : (u + 1) * UNIT],
                    start=True,
                    stop=True,
                )
            interleaved = h_grouped[g][:, place * UNIT : (place + 1) * UNIT, :]
            sums = bank[:].rearrange("p t n -> p n t")
            if place == 0 and g in VECTOR_GROUPS:
                nc.vector.tensor_scalar_max(interleaved, sums, 0.0)
            else:
                nc.scalar.activation(interleaved, sums, ACT.Relu)

        def quantize_h(g):
            if g == groups - 1:
                tag = f"h_grouped{g - 1}"
            elif g >= REUSE_LAG:
                tag = f"activated{g - REUSE_LAG}"
            else:
                tag = f"h_codes{g}"
            h_codes[g] = held.tile([P, GROUP], U32, name=f"h_codes{g}", tag=tag, align_bytes=256)
            nc.vector.quantize_mx(
                out=h_codes[g][:].bitcast(FP8X4),
                scales=h_scale_tile[g][:],
                in_=h_grouped[g][:].rearrange("p n t -> p (n t)"),
            )

        def pieces(g):
            width = UNIT if g == groups - 1 else GROUP
            return [slice(c0, c0 + width) for c0 in range(0, GROUP, width)]

        def second_layer(g):
            for cols in pieces(g):
                if g == groups - 1:
                    free_tag = bank_tag((g * GROUP + cols.start) // UNIT)
                    y_banks[g, cols.start] = h_psum.tile([P, GROUP], F32, name=f"last_y_bank{cols.start}", tag=free_tag)
                else:
                    y_banks[g, cols.start] = y_psum.tile([P, GROUP], F32, name="y_bank")
                nc.tensor.matmul_mx(
                    out=y_banks[g, cols.start][:, cols],
                    lhsT=w2_codes[:].bitcast(FP4X4),
                    lhsT_scale=w2_scale_tile[:].bitcast(U8),
                    rhs=h_codes[g][:, cols].bitcast(FP8X4),
                    rhs_scale=h_scale_tile[g][:, cols],
                    start=True,
                    stop=True,
                )

        def gelu(g):
            activated[g] = held.tile([P, GROUP], F32, name=f"activated{g}", tag=f"activated{g}", align_bytes=256)
            for cols in pieces(g):
                nc.scalar.activation(activated[g][:, cols], y_banks[g, cols.start][:, cols], ACT.Gelu_apprx_tanh, bias=bias[:])

        def gate_and_store(g):
            for cols in pieces(g):
                s0, s1 = g * GROUP + cols.start, g * GROUP + cols.stop
                nc.vector.tensor_tensor(
                    result[g][:, cols], gates[:].indirect(list_slice(s0, s1)), activated[g][:, cols], ALU.mult
                )
                nc.sync.dma_start(out[:, s0:s1], result[g][:, cols])

        units = S // UNIT
        group_ending_at = {(g + 1) * GROUP_UNITS - 1: g for g in range(groups)}

        def finish(first, end):
            for g in range(first, end):
                gelu(g)
                gate_and_store(g)

        for step in range(units):
            first_layer(step)
            if step == units - 1:
                late_tag = bank_tag(units - GROUP_UNITS - 1)
                warm_up(LATE_WARM_PASSES, h_psum.tile([P, WARM_N], F32, name="late_bank", tag=late_tag), picked_words[0])
            if step in group_ending_at:
                g = group_ending_at[step]
                if g == REUSE_LAG:
                    finish(0, REUSE_LAG - 1)
                quantize_h(g)
                second_layer(g)
                if g == groups - 2:
                    finish(REUSE_LAG - 1, REUSE_LAG)
        finish(REUSE_LAG, groups)
